import numpy as np
import ml_dtypes


def mxq(x, axis, fmt="e4m3"):
    dtype, down = {"e4m3": (ml_dtypes.float8_e4m3fn, 7), "e5m2": (ml_dtypes.float8_e5m2, 14)}[fmt]
    v = np.moveaxis(np.asarray(x, np.float32).astype(ml_dtypes.bfloat16).astype(np.float64), axis, -1)
    blocks = v.reshape(v.shape[:-1] + (-1, 32))
    amax = np.abs(blocks).max(-1, keepdims=True)
    byte = np.maximum(np.where(amax > 0, np.frexp(amax)[1] - 1 + 127, 0) - down, 1)
    scale = np.exp2(byte - 127.0)
    codes = (blocks / scale).astype(np.float32).astype(dtype).astype(np.float64)
    return np.moveaxis((codes * scale).reshape(v.shape), -1, axis)


WIDE = False


def mx_kscale(k):
    if not WIDE:
        return np.ones(k)
    levels = np.array([10, -10, 5, -5, 0])
    if k % 512:
        return np.exp2(np.random.permutation(np.resize(levels, k // 32))).repeat(32)
    a = np.empty((k // 512, 16))
    for p in range(k // 512):
        a[p, :8] = np.random.permutation(np.resize(levels, 8))
        for g in range(8):
            far = levels[np.abs(levels - a[p, g]) >= 10]
            a[p, g + 8] = far[np.random.randint(len(far))]
    return np.exp2(a.ravel()).repeat(32)


def f64(x):
    return np.asarray(x).astype(np.float64)


def striped(idx):
    return np.tile(idx.reshape(-1, 16).T, (8, 1)).astype(np.uint16)


def unstriped(offs):
    return offs[:16].T.reshape(-1).astype(np.int64)


E2M1 = np.array([0.0, 0.5, 1.0, 1.5, 2.0, 3.0, 4.0, 6.0, -0.0, -0.5, -1.0, -1.5, -2.0, -3.0, -4.0, -6.0])


def pack_weight(w, fmt):
    k, n = w.shape
    w = f64(np.asarray(w, np.float32).astype(ml_dtypes.bfloat16)).reshape(k // 32, 32, n)
    amax = np.abs(w).max(1)
    if fmt == "e4m3":
        byte = np.frexp(amax)[1] - 1 + 127 - 7
    else:
        mant, ex = np.frexp(amax / 6.0)
        byte = np.where(mant > 0.5, ex, ex - 1) + 127
    byte = np.clip(np.where(amax > 0, byte, 1), 1, 254)
    scaled = (w * np.exp2(127.0 - byte)[:, None, :]).reshape(k, n).astype(np.float32)
    by_word = np.ascontiguousarray(scaled.reshape(k // 512, 128, 4, n).transpose(0, 1, 3, 2))
    if fmt == "e4m3":
        words = by_word.astype(ml_dtypes.float8_e4m3fn).view(np.uint8)
    else:
        c = by_word.astype(ml_dtypes.float4_e2m1fn).view(np.uint8) & 0xF
        words = (c[..., 0::2] | (c[..., 1::2] << 4)).reshape(k // 512, 128, 2 * n)
    return np.ascontiguousarray(words), np.ascontiguousarray(byte.astype(np.uint8).reshape(k // 512, 16, n))


def unpack_weight(words, scales, fmt):
    g, _, n = scales.shape
    words = np.ascontiguousarray(words).reshape(g, 128, n, -1)
    if fmt == "e4m3":
        vals = words.view(ml_dtypes.float8_e4m3fn).astype(np.float64)
    else:
        nib = np.empty((g, 128, n, 4), np.uint8)
        nib[..., 0::2] = words & 0xF
        nib[..., 1::2] = words >> 4
        vals = E2M1[nib]
    vals = vals * np.repeat(np.exp2(scales.astype(np.float64) - 127.0), 8, axis=1)[..., None]
    return vals.transpose(0, 1, 3, 2).reshape(g * 512, n)


def gelu(v):
    return 0.5 * v * (1.0 + np.tanh(np.sqrt(2.0 / np.pi) * (v + 0.044715 * v**3)))


K, K2, H, N, T, S, T2 = 1024, 512, 1024, 512, 2048, 512, 1024

def setup_inputs():
    n = np.random.standard_normal
    s, s2, u = mx_kscale(K)[:, None], mx_kscale(K2)[:, None], mx_kscale(H)[:, None]
    tab_words, tab_scales = pack_weight(n((K, T)) * s, "e4m3")
    tab2_words, tab2_scales = pack_weight(n((K2, T)) * s2, "e4m3")
    w2_words, w2_scales = pack_weight(n((K, H)) / np.sqrt(K) / s, "e2m1")
    w4_words, w4_scales = pack_weight(n((H, N)) / np.sqrt(H) / u, "e2m1")
    return {
        "tab_words": tab_words, "tab_scales": tab_scales,
        "tab2_words": tab2_words, "tab2_scales": tab2_scales,
        "offs": striped(np.random.permutation(T)[:S]),
        "offs2": striped(np.random.permutation(T)[:S]),
        "offs3": striped(np.random.permutation(T2)[:S]),
        "offs4": striped(np.random.permutation(T2)[:S]),
        "w1": (n((K, H)) / np.sqrt(K) / s).astype(np.float32),
        "w2_words": w2_words, "w2_scales": w2_scales,
        "b1": (0.6 * n(H)).astype(np.float32),
        "w3": (1.6 * n((K2, H)) / np.sqrt(K2) / s2).astype(np.float32),
        "wg1": np.exp(0.3 * n((128, S))).astype(np.float32),
        "wg2": np.exp(0.3 * n((128, S))).astype(np.float32),
        "hyd": (0.6 * n((H, T2))).astype(np.float32),
        "cal": (np.exp(0.3 * n(H)) * u[:, 0]).astype(np.float32),
        "w4_words": w4_words, "w4_scales": w4_scales,
        "res": (0.5 * n((N, T2))).astype(np.float32),
    }

def reference(tab_words, tab_scales, tab2_words, tab2_scales, offs, offs2, offs3, offs4, w1, w2_words, w2_scales, b1, w3, wg1, wg2, hyd, cal, w4_words, w4_scales, res):
    v = unpack_weight(tab_words, tab_scales, "e4m3")[:, unstriped(offs)]
    v2 = unpack_weight(tab2_words, tab2_scales, "e4m3")[:, unstriped(offs2)]
    h1 = (mxq(f64(w1), 0, "e4m3").T @ v) * (unpack_weight(w2_words, w2_scales, "e2m1").T @ v) + f64(b1)[:, None]
    h2 = np.tanh(mxq(f64(w3), 0, "e4m3").T @ v2)
    pa = np.zeros((H, T2))
    pa[:, unstriped(offs3)] = np.tile(f64(wg1), (H // 128, 1)) * h1
    pb = np.zeros((H, T2))
    pb[:, unstriped(offs4)] = np.tile(f64(wg2), (H // 128, 1)) * h2
    z = np.maximum(pa, pb) + f64(hyd)
    x = z * f64(cal)[:, None]
    return (unpack_weight(w4_words, w4_scales, "e2m1").T @ mxq(x, 0, "e4m3")) + f64(res)

@@ -1,0 +1,342 @@
+from contextlib import ExitStack
+
+import concourse.mybir as mybir
+from concourse.masks import make_identity
+
+F32 = mybir.dt.float32
+BF16 = mybir.dt.bfloat16
+I32 = mybir.dt.int32
+U32 = mybir.dt.uint32
+U16 = mybir.dt.uint16
+U8 = mybir.dt.uint8
+FP8X4 = mybir.dt.float8_e4m3fn_x4
+FP4X4 = mybir.dt.float4_e2m1fn_x4
+ALU = mybir.AluOpType
+ACT = mybir.ActivationFunctionType
+
+FLOPS = 3758096384
+
+P = 128
+T = 2048
+S = 512
+M = 1024
+HALF = 512
+SLICES = 8
+LAST = SLICES - 1
+TAIL_VECTOR_COLS = 320
+
+
+def tile_list_gravimetry_storage_score_kernel(
+    tc, tab_words, tab_scales, tab2_words, tab2_scales, offs, offs2, offs3, offs4,
+    w1, w2_words, w2_scales, b1, w3, wg1, wg2, hyd, cal, w4_words, w4_scales, res, out,
+):
+    nc = tc.nc
+    with ExitStack() as ctx:
+        keep = ctx.enter_context(tc.tile_pool(name="keep", bufs=1))
+        ring = ctx.enter_context(tc.tile_pool(name="ring", bufs=2))
+        psum = ctx.enter_context(tc.psum_pool(name="psum", bufs=1))
+
+        def held(name, shape, dtype):
+            return keep.tile(shape, dtype, name=name, align_bytes=64)
+
+        def bank(index, name, shape):
+            return psum.tile(shape, F32, name=name, tag="bank%d" % index)
+
+        tab2_sc = held("tab2_sc", [P, T], U8)
+        tab_sc = held("tab_sc", [P, 2 * T], U8)
+        w2_sc_raw = held("w2_sc_raw", [P, 2 * 1024], U8)
+        w4_sc = held("w4_sc", [P, 2 * 512], U8)
+        page_b = [held("page_b%d" % i, [P, M], F32) for i in range(5)]
+        page_a = [held("page_a%d" % i, [P, M], F32) for i in range(2)]
+        nc.vector.memset(tab2_sc[:].bitcast(I32), 0)
+        nc.vector.memset(tab_sc[:].bitcast(I32), 0)
+        nc.vector.memset(w2_sc_raw[:].bitcast(I32), 0)
+        nc.vector.memset(w4_sc[:].bitcast(I32), 0)
+        nc.vector.memset(page_b[0][:], 0.0)
+        ident = held("ident", [P, P], F32)
+        make_identity(nc, ident[:])
+
+        def load_list(name, src):
+            tile = keep.tile([P, S // 16], U16, name=name)
+            nc.sync.dma_start(tile[:], src)
+            return tile
+
+        def stream(name, shape, src):
+            tile = ring.tile(shape, F32, name=name, tag="stream", bufs=6)
+            nc.sync.dma_start(tile[:], src)
+            return tile
+
+        def load_weight(name, w, a, b):
+            src = w[512 * a:512 * (a + 1), 512 * b:512 * (b + 1)].rearrange("(p j) c -> p j c", j=4)
+            return stream(name, [P, 4, 512], src)
+
+        def load_hyd(pair):
+            b, t0 = divmod(2 * pair, 4)
+            src = hyd[512 * b:512 * (b + 1), :].rearrange("(p t) m -> p t m", t=4)[:, t0:t0 + 2, :]
+            return stream("hyd%d" % pair, [P, 2, M], src)
+
+        def load_words(name, src):
+            tile = held(name, [P, T], U32)
+            nc.sync.dma_start(tile[:].bitcast(I32), src.rearrange("p c i -> p (c i)").bitcast(I32))
+            return tile
+
+        def load_scales(tile, src):
+            passes = src.shape[0]
+            for q in range(4):
+                dst = tile[32 * q:32 * q + 4, :].bitcast(I32).rearrange("r (a c) -> r a c", a=passes)
+                nc.sync.dma_start(dst, src[:, 4 * q:4 * q + 4, :].rearrange("a r c -> r a c").bitcast(I32))
+
+        def load_gain(name, src, t0, t1):
+            tile = held(name, [P, t1 - t0, S], F32)
+            rows = src.rearrange("(v t) j -> v t j", t=4)[:, t0:t1, :]
+            for u in (0, 2, 1, 3):
+                nc.sync.dma_start(tile[32 * u:32 * (u + 1), :, :], rows)
+            return [tile[:, t, :] for t in range(t1 - t0)]
+
+        def load_rowwise(name, src):
+            tile = held(name, [P, 2, 4], F32)
+            nc.sync.dma_start(tile[:], src.rearrange("(b p t) -> p b t", b=2, t=4))
+            return tile[:].rearrange("p b t -> p (b t)")
+
+        idx2 = load_list("idx2", offs2)
+        idx4 = load_list("idx4", offs4)
+        w3_raw = [load_weight("w3_raw0", w3, 0, 0)]
+        tab2_w = load_words("tab2_w", tab2_words[0])
+        load_scales(tab2_sc, tab2_scales)
+        gain2 = load_gain("gain2_0", wg2, 0, 1)
+        gain2 = gain2 + load_gain("gain2_1", wg2, 1, 2)
+        idx = load_list("idx", offs)
+        tab_w = [load_words("tab_w%d" % a, tab_words[a]) for a in range(2)]
+        load_scales(tab_sc, tab_scales)
+        gain2 = gain2 + load_gain("gain2_2", wg2, 2, 3)
+        w1_raw = {(a, 0): load_weight("w1_raw%d0" % a, w1, a, 0) for a in range(2)}
+        w2_raw = held("w2_raw", [P, 2 * 2048], U8)
+        nc.sync.dma_start(
+            w2_raw[:].bitcast(I32).rearrange("p (a c) -> p a c", a=2),
+            w2_words.rearrange("a p c -> p a c").bitcast(I32),
+        )
+        load_scales(w2_sc_raw, w2_scales)
+        idx3 = load_list("idx3", offs3)
+        bias = load_rowwise("bias", b1)
+        factor = load_rowwise("factor", cal)
+        gain1 = load_gain("gain1_0", wg1, 0, 1)
+        gain2 = gain2 + load_gain("gain2_3", wg2, 3, 4)
+        hyd_pairs = [load_hyd(0)]
+        w3_raw.append(load_weight("w3_raw1", w3, 0, 1))
+        gain1 = gain1 + load_gain("gain1_1", wg1, 1, 4)
+        for a in range(2):
+            w1_raw[a, 1] = load_weight("w1_raw%d1" % a, w1, a, 1)
+        hyd_pairs.extend(load_hyd(pair) for pair in range(1, 4))
+        w4_w = held("w4_w", [P, 2 * 1024], U8)
+        nc.sync.dma_start(
+            w4_w[:].bitcast(I32).rearrange("p (a c) -> p a c", a=2),
+            w4_words.rearrange("a p c -> p a c").bitcast(I32),
+        )
+        load_scales(w4_sc, w4_scales)
+        res_pairs = [
+            stream("res%d" % k, [P, 2, M], res[256 * k:256 * (k + 1), :].rearrange("(g p) m -> p g m", p=P))
+            for k in range(2)
+        ]
+
+        neg_bias = held("neg_bias", [P, SLICES], F32)
+        nc.vector.tensor_scalar(neg_bias[:], bias, -1.0, None, ALU.mult)
+
+        def gather(name, dtype, window, offsets):
+            tile = held(name, [P, S], dtype)
+            nc.vector.tensor_copy(tile[:], window.indirect(offsets[:]))
+            return tile
+
+        def quantise_weight(name, raw, on_vector):
+            grouped = ring.tile([P, 2048], BF16, name=name + "_bf", tag="grouped", align_bytes=64)
+            dst = grouped[:].rearrange("p (t m j) -> p m j t", t=4, j=4)
+            src = raw[:].rearrange("p j (m t) -> p m j t", t=4)
+            if on_vector:
+                nc.vector.tensor_copy(dst, src)
+            else:
+                nc.scalar.copy(dst, src)
+            codes = held(name + "_codes", [P, 512], U32)
+            scales = held(name + "_scales", [P, 512], U8)
+            nc.vector.quantize_mx(out=codes[:].bitcast(FP8X4), scales=scales[:], in_=grouped[:])
+            return codes, scales
+
+        def deal_w2(b):
+            words = held("w2_w%d" % b, [P, 2 * 1024], U8)
+            scales = held("w2_sc%d" % b, [P, 2 * 512], U8)
+            nc.vector.tensor_copy(
+                words[:].bitcast(U16).rearrange("p (a t q) -> p a t q", a=2, t=4),
+                w2_raw[:].bitcast(U16).rearrange("p (a b q t) -> p b a t q", a=2, b=2, t=4)[:, b],
+            )
+            nc.vector.tensor_copy(
+                scales[:].rearrange("p (a t q) -> p a t q", a=2, t=4),
+                w2_sc_raw[:].rearrange("p (a b q t) -> p b a t q", a=2, b=2, t=4)[:, b],
+            )
+            return words, scales
+
+        w3_q = {0: quantise_weight("w3_0", w3_raw[0], True)}
+        v2_w = gather("v2_w", U32, tab2_w[:], idx2)
+        v2_sc = gather("v2_sc", U8, tab2_sc[:], idx2)
+
+        for page in page_b[1:] + page_a:
+            nc.vector.memset(page[:], 0.0)
+
+        def place_b(s):
+            b, t = divmod(s, 4)
+            cols = slice(P * t, P * (t + 1))
+            acc = bank(2, "sum3_%d" % s, [P, S])
+            nc.tensor.matmul_mx(
+                out=acc[:], lhsT=w3_q[b][0][:, cols].bitcast(FP8X4), lhsT_scale=w3_q[b][1][:, cols],
+                rhs=v2_w[:].bitcast(FP8X4), rhs_scale=v2_sc[:], start=True, stop=True,
+            )
+            h2 = ring.tile([P, S], F32, name="h2_%d" % s, tag="h2", bufs=3)
+            nc.scalar.activation(h2[:], acc[:], ACT.Tanh)
+            nc.vector.tensor_tensor(page_b[s % 5][:].indirect(idx4[:]), h2[:], gain2[t], ALU.mult)
+
+        place_b(0)
+        place_b(1)
+        v_w = [gather("v_w%d" % a, U32, tab_w[a][:], idx) for a in range(2)]
+        v_sc = [gather("v_sc%d" % a, U8, tab_sc[:, T * a:T * (a + 1)], idx) for a in range(2)]
+        place_b(2)
+        w1_q = {(a, 0): quantise_weight("w1_%d0" % a, w1_raw[a, 0], False) for a in range(2)}
+        w2_q = {0: deal_w2(0)}
+
+        def make_h1(s):
+            b, t = divmod(s, 4)
+            cols = slice(P * t, P * (t + 1))
+            acc1 = bank(0, "sum1_%d" % s, [P, S])
+            acc2 = bank(1, "sum2_%d" % s, [P, S])
+            for a in range(2):
+                nc.tensor.matmul_mx(
+                    out=acc1[:], lhsT=w1_q[a, b][0][:, cols].bitcast(FP8X4), lhsT_scale=w1_q[a, b][1][:, cols],
+                    rhs=v_w[a][:].bitcast(FP8X4), rhs_scale=v_sc[a][:], start=(a == 0), stop=(a == 1),
+                )
+            for a in range(2):
+                c0 = 512 * a + P * t
+                nc.tensor.matmul_mx(
+                    out=acc2[:], lhsT=w2_q[b][0][:, 2 * c0:2 * (c0 + P)].bitcast(FP4X4),
+                    lhsT_scale=w2_q[b][1][:, c0:c0 + P],
+                    rhs=v_w[a][:].bitcast(FP8X4), rhs_scale=v_sc[a][:], start=(a == 0), stop=(a == 1),
+                )
+            first = ring.tile([P, S], F32, name="first_%d" % s, tag="first")
+            nc.scalar.copy(first[:], acc1[:])
+            product = ring.tile([P, S], F32, name="product_%d" % s, tag="product")
+            nc.vector.tensor_tensor(product[:], acc2[:], first[:], ALU.mult)
+            h1 = ring.tile([P, S], F32, name="h1_%d" % s, tag="h1", bufs=3)
+            if s == LAST:
+                nc.scalar.activation(h1[:], product[:], ACT.Identity, bias=bias[:, s:s + 1], scale=1.0)
+            else:
+                nc.scalar.activation(h1[:], product[:], ACT.Identity, bias=neg_bias[:, s:s + 1], scale=-1.0)
+            return h1
+
+        def place_a(s, h1):
+            nc.vector.tensor_tensor(page_a[s % 2][:].indirect(idx3[:]), h1[:], gain1[s % 4], ALU.mult)
+
+        turn = []
+
+        def add_transposed(name, first, second):
+            acc = bank(3 + len(turn) % 5, name, [P, 4, P])
+            turn.append(name)
+            for k in range(4):
+                nc.tensor.matmul(acc[:, k, :], first(k), ident[:], start=True, stop=False, is_transpose=True)
+                nc.tensor.matmul(acc[:, k, :], second(k), ident[:], start=False, stop=True, is_transpose=True)
+            return acc
+
+        def block(rows, h):
+            return lambda k: rows[:, HALF * h + P * k:HALF * h + P * (k + 1)]
+
+        def base_sum(s, h):
+            acc = add_transposed("base_%d_%d" % (s, h), block(page_b[s % 5], h), block(hyd_pairs[s // 2][:, s % 2, :], h))
+            base = ring.tile([P, 4, P], F32, name="base_sb_%d_%d" % (s, h), tag="base", bufs=4)
+            nc.scalar.copy(base[:], acc[:])
+            return base
+
+        def excess(s, h):
+            acc = add_transposed("diff_%d_%d" % (s, h), block(page_a[s % 2], h), block(page_b[s % 5], h))
+            over = ring.tile([P, 4, P], F32, name="over_%d_%d" % (s, h), tag="over", bufs=3)
+            nc.scalar.activation(over[:], acc[:], ACT.Relu, scale=-1.0)
+            return over
+
+        planes = [held("planes%d" % b, [P, 4, M], BF16) for b in range(2)]
+
+        def finish_plane(s, h, base, over):
+            acc = add_transposed("z_%d_%d" % (s, h), lambda k: over[:, k, :], lambda k: base[:, k, :])
+            nc.scalar.activation(
+                planes[s // 4][:, s % 4, HALF * h:HALF * (h + 1)], acc[:].rearrange("p k c -> p (k c)"),
+                ACT.Copy, scale=factor[:, s:s + 1],
+            )
+
+        def weave(engine_copy, woven, b, h, c0, c1):
+            dst = woven[:, 4 * c0:4 * c1].rearrange("p (c i t) -> p c t i", i=4, t=4)
+            src = planes[b][:, :, HALF * h + c0:HALF * h + c1].rearrange("p t (c i) -> p c t i", i=4)
+            engine_copy(dst, src)
+
+        x_q = {}
+
+        def quantise_x(b, h, vector_cols):
+            woven = ring.tile([P, 4 * HALF], BF16, name="woven_%d_%d" % (b, h), tag="woven", align_bytes=64)
+            if vector_cols > 0:
+                weave(nc.vector.tensor_copy, woven, b, h, 0, vector_cols)
+            if vector_cols < HALF:
+                weave(nc.scalar.copy, woven, b, h, vector_cols, HALF)
+            codes = held("x_codes_%d_%d" % (b, h), [P, HALF], U32)
+            scales = held("x_scales_%d_%d" % (b, h), [P, HALF], U8)
+            nc.vector.quantize_mx(out=codes[:].bitcast(FP8X4), scales=scales[:], in_=woven[:])
+            x_q[b, h] = (codes, scales)
+
+        h1_next = make_h1(0)
+        place_b(3)
+        for s in range(LAST):
+            h1_now = h1_next
+            if s == 0:
+                w3_q[1] = quantise_weight("w3_1", w3_raw[1], False)
+            if s in (1, 2):
+                w1_q[s - 1, 1] = quantise_weight("w1_%d1" % (s - 1), w1_raw[s - 1, 1], False)
+            if s == 2:
+                w2_q[1] = deal_w2(1)
+            h1_next = make_h1(s + 1)
+            bases = [base_sum(s, h) for h in range(2)]
+            place_a(s, h1_now)
+            overs = [excess(s, h) for h in range(2)]
+            if s + 4 < SLICES:
+                place_b(s + 4)
+            for h in range(2):
+                finish_plane(s, h, bases[h], overs[h])
+            if s == 3:
+                quantise_x(0, 0, 0)
+                quantise_x(0, 1, HALF)
+
+        hyd_last = hyd_pairs[LAST // 2][:, LAST % 2, :]
+        nc.scalar.activation(hyd_last, hyd_last, ACT.Copy, scale=factor[:, LAST:LAST + 1])
+        place_a(LAST, h1_next)
+        larger = []
+        for h in range(2):
+            cols = slice(HALF * h, HALF * (h + 1))
+            top = ring.tile([P, HALF], F32, name="larger_%d" % h, tag="over", bufs=3)
+            nc.vector.tensor_tensor(top[:], page_a[LAST % 2][:, cols], page_b[LAST % 5][:, cols], ALU.max)
+            larger.append(top)
+        for h in range(2):
+            cols = slice(HALF * h, HALF * (h + 1))
+            nc.vector.scalar_tensor_tensor(
+                planes[1][:, 3, cols], larger[h][:], factor[:, LAST:LAST + 1], hyd_last[:, cols], ALU.mult, ALU.add,
+            )
+        for h in range(2):
+            quantise_x(1, h, TAIL_VECTOR_COLS)
+
+        sums = {}
+        for b in range(2):
+            for h in range(2):
+                for g in range(4):
+                    if b == 0:
+                        sums[h, g] = bank(4 * h + g, "out_%d_%d" % (h, g), [P, HALF])
+                    c0 = 512 * b + P * g
+                    nc.tensor.matmul_mx(
+                        out=sums[h, g][:], lhsT=w4_w[:, 2 * c0:2 * (c0 + P)].bitcast(FP4X4),
+                        lhsT_scale=w4_sc[:, c0:c0 + P],
+                        rhs=x_q[b, h][0][:].bitcast(FP8X4), rhs_scale=x_q[b, h][1][:],
+                        start=(b == 0), stop=(b == 1),
+                    )
+        for h in range(2):
+            cols = slice(HALF * h, HALF * (h + 1))
+            for g in range(4):
+                rows = res_pairs[g // 2][:, g % 2, cols]
+                nc.vector.tensor_tensor(rows, sums[h, g][:], rows, ALU.add)
+                nc.sync.dma_start(out[P * g:P * (g + 1), cols], rows)

@@ -1,7 +1,6 @@
 from contextlib import ExitStack
 
 import concourse.mybir as mybir
-from concourse.masks import make_identity
 
 F32 = mybir.dt.float32
 BF16 = mybir.dt.bfloat16
@@ -24,6 +23,7 @@ HALF = 512
 SLICES = 8
 LAST = SLICES - 1
 TAIL_VECTOR_COLS = 320
+PRODUCT_ON_VECTOR = (0, 6, 7)
 
 
 def tile_list_gravimetry_storage_score_kernel(
@@ -47,14 +47,12 @@ def tile_list_gravimetry_storage_score_kernel(
         w2_sc_raw = held("w2_sc_raw", [P, 2 * 1024], U8)
         w4_sc = held("w4_sc", [P, 2 * 512], U8)
         page_b = [held("page_b%d" % i, [P, M], F32) for i in range(5)]
-        page_a = [held("page_a%d" % i, [P, M], F32) for i in range(2)]
-        nc.vector.memset(tab2_sc[:].bitcast(I32), 0)
-        nc.vector.memset(tab_sc[:].bitcast(I32), 0)
+        page_a = held("page_a", [P, M], F32)
+        nc.gpsimd.memset(tab2_sc[:].bitcast(I32), 0)
+        nc.gpsimd.memset(tab_sc[:].bitcast(I32), 0)
         nc.vector.memset(w2_sc_raw[:].bitcast(I32), 0)
         nc.vector.memset(w4_sc[:].bitcast(I32), 0)
         nc.vector.memset(page_b[0][:], 0.0)
-        ident = held("ident", [P, P], F32)
-        make_identity(nc, ident[:])
 
         def load_list(name, src):
             tile = keep.tile([P, S // 16], U16, name=name)
@@ -62,7 +60,7 @@ def tile_list_gravimetry_storage_score_kernel(
             return tile
 
         def stream(name, shape, src):
-            tile = ring.tile(shape, F32, name=name, tag="stream", bufs=6)
+            tile = ring.tile(shape, F32, name=name, tag="stream", bufs=7)
             nc.sync.dma_start(tile[:], src)
             return tile
 
@@ -86,60 +84,64 @@ def tile_list_gravimetry_storage_score_kernel(
                 dst = tile[32 * q:32 * q + 4, :].bitcast(I32).rearrange("r (a c) -> r a c", a=passes)
                 nc.sync.dma_start(dst, src[:, 4 * q:4 * q + 4, :].rearrange("a r c -> r a c").bitcast(I32))
 
-        def load_gain(name, src, t0, t1):
-            tile = held(name, [P, t1 - t0, S], F32)
-            rows = src.rearrange("(v t) j -> v t j", t=4)[:, t0:t1, :]
+        def load_gain(name, src, t):
+            tile = held(name, [P, S], F32)
+            rows = src.rearrange("(v t) j -> v t j", t=4)[:, t, :]
             for u in (0, 2, 1, 3):
-                nc.sync.dma_start(tile[32 * u:32 * (u + 1), :, :], rows)
-            return [tile[:, t, :] for t in range(t1 - t0)]
+                nc.sync.dma_start(tile[32 * u:32 * (u + 1), :], rows)
+            return tile[:]
+
+        def load_fp4_words(name, src):
+            tile = held(name, [P, 2 * src.shape[2]], U8)
+            nc.sync.dma_start(
+                tile[:].bitcast(I32).rearrange("p (a c) -> p a c", a=2),
+                src.rearrange("a p c -> p a c").bitcast(I32),
+            )
+            return tile
+
+        def load_res(pair):
+            src = res[256 * pair:256 * (pair + 1), :].rearrange("(g p) m -> p g m", p=P)
+            return stream("res%d" % pair, [P, 2, M], src)
 
         def load_rowwise(name, src):
             tile = held(name, [P, 2, 4], F32)
             nc.sync.dma_start(tile[:], src.rearrange("(b p t) -> p b t", b=2, t=4))
             return tile[:].rearrange("p b t -> p (b t)")
 
+        w1_raw, w3_raw, gain1, gain2, hyd_pairs = {}, {}, {}, {}, {}
         idx2 = load_list("idx2", offs2)
         idx4 = load_list("idx4", offs4)
-        w3_raw = [load_weight("w3_raw0", w3, 0, 0)]
+        idx = load_list("idx", offs)
+        w3_raw[0] = load_weight("w3_raw0", w3, 0, 0)
         tab2_w = load_words("tab2_w", tab2_words[0])
         load_scales(tab2_sc, tab2_scales)
-        gain2 = load_gain("gain2_0", wg2, 0, 1)
-        gain2 = gain2 + load_gain("gain2_1", wg2, 1, 2)
-        idx = load_list("idx", offs)
+        gain2[0] = load_gain("gain2_0", wg2, 0)
+        gain2[1] = load_gain("gain2_1", wg2, 1)
         tab_w = [load_words("tab_w%d" % a, tab_words[a]) for a in range(2)]
         load_scales(tab_sc, tab_scales)
-        gain2 = gain2 + load_gain("gain2_2", wg2, 2, 3)
-        w1_raw = {(a, 0): load_weight("w1_raw%d0" % a, w1, a, 0) for a in range(2)}
-        w2_raw = held("w2_raw", [P, 2 * 2048], U8)
-        nc.sync.dma_start(
-            w2_raw[:].bitcast(I32).rearrange("p (a c) -> p a c", a=2),
-            w2_words.rearrange("a p c -> p a c").bitcast(I32),
-        )
+        gain2[2] = load_gain("gain2_2", wg2, 2)
+        w2_raw = load_fp4_words("w2_raw", w2_words)
         load_scales(w2_sc_raw, w2_scales)
-        idx3 = load_list("idx3", offs3)
+        w1_raw[0, 0] = load_weight("w1_raw00", w1, 0, 0)
+        w1_raw[1, 0] = load_weight("w1_raw10", w1, 1, 0)
+        gain2[3] = load_gain("gain2_3", wg2, 3)
         bias = load_rowwise("bias", b1)
+        idx3 = load_list("idx3", offs3)
+        gain1[0] = load_gain("gain1_0", wg1, 0)
+        w3_raw[1] = load_weight("w3_raw1", w3, 0, 1)
+        gain1[1] = load_gain("gain1_1", wg1, 1)
         factor = load_rowwise("factor", cal)
-        gain1 = load_gain("gain1_0", wg1, 0, 1)
-        gain2 = gain2 + load_gain("gain2_3", wg2, 3, 4)
-        hyd_pairs = [load_hyd(0)]
-        w3_raw.append(load_weight("w3_raw1", w3, 0, 1))
-        gain1 = gain1 + load_gain("gain1_1", wg1, 1, 4)
-        for a in range(2):
-            w1_raw[a, 1] = load_weight("w1_raw%d1" % a, w1, a, 1)
-        hyd_pairs.extend(load_hyd(pair) for pair in range(1, 4))
-        w4_w = held("w4_w", [P, 2 * 1024], U8)
-        nc.sync.dma_start(
-            w4_w[:].bitcast(I32).rearrange("p (a c) -> p a c", a=2),
-            w4_words.rearrange("a p c -> p a c").bitcast(I32),
-        )
+        hyd_pairs[0] = load_hyd(0)
+        gain1[2] = load_gain("gain1_2", wg1, 2)
+        w1_raw[0, 1] = load_weight("w1_raw01", w1, 0, 1)
+        gain1[3] = load_gain("gain1_3", wg1, 3)
+        w1_raw[1, 1] = load_weight("w1_raw11", w1, 1, 1)
+        hyd_pairs[1] = load_hyd(1)
+        w4_w = load_fp4_words("w4_w", w4_words)
         load_scales(w4_sc, w4_scales)
-        res_pairs = [
-            stream("res%d" % k, [P, 2, M], res[256 * k:256 * (k + 1), :].rearrange("(g p) m -> p g m", p=P))
-            for k in range(2)
-        ]
-
-        neg_bias = held("neg_bias", [P, SLICES], F32)
-        nc.vector.tensor_scalar(neg_bias[:], bias, -1.0, None, ALU.mult)
+        hyd_pairs[2] = load_hyd(2)
+        hyd_pairs[3] = load_hyd(3)
+        res_pairs = [load_res(pair) for pair in range(2)]
 
         def gather(name, dtype, window, offsets):
             tile = held(name, [P, S], dtype)
@@ -160,50 +162,65 @@ def tile_list_gravimetry_storage_score_kernel(
             return codes, scales
 
         def deal_w2(b):
-            words = held("w2_w%d" % b, [P, 2 * 1024], U8)
-            scales = held("w2_sc%d" % b, [P, 2 * 512], U8)
-            nc.vector.tensor_copy(
-                words[:].bitcast(U16).rearrange("p (a t q) -> p a t q", a=2, t=4),
-                w2_raw[:].bitcast(U16).rearrange("p (a b q t) -> p b a t q", a=2, b=2, t=4)[:, b],
-            )
-            nc.vector.tensor_copy(
-                scales[:].rearrange("p (a t q) -> p a t q", a=2, t=4),
-                w2_sc_raw[:].rearrange("p (a b q t) -> p b a t q", a=2, b=2, t=4)[:, b],
-            )
+            words = keep.tile([P, 2 * 1024], U8, name="w2_w%d" % b, tag="w2_w%d" % b, align_bytes=64)
+            scales = keep.tile([P, 2 * 512], U8, name="w2_sc%d" % b, tag="w2_sc%d" % b, align_bytes=64)
+            word_src = w2_raw[:].rearrange("p (a b q t e) -> p a b t q e", a=2, b=2, t=4, e=2)
+            scale_src = w2_sc_raw[:].rearrange("p (a b q t) -> p b a t q", a=2, b=2, t=4)
+            for a in range(2):
+                nc.gpsimd.tensor_copy(
+                    words[:, 1024 * a:1024 * (a + 1)].rearrange("p (t q e) -> p t q e", t=4, e=2), word_src[:, a, b],
+                )
+            nc.gpsimd.tensor_copy(scales[:].rearrange("p (a t q) -> p a t q", a=2, t=4), scale_src[:, b])
             return words, scales
 
         w3_q = {0: quantise_weight("w3_0", w3_raw[0], True)}
         v2_w = gather("v2_w", U32, tab2_w[:], idx2)
         v2_sc = gather("v2_sc", U8, tab2_sc[:], idx2)
 
-        for page in page_b[1:] + page_a:
+        for page in page_b[1:] + [page_a]:
             nc.vector.memset(page[:], 0.0)
 
-        def place_b(s):
+        def make_h2(s):
             b, t = divmod(s, 4)
             cols = slice(P * t, P * (t + 1))
-            acc = bank(2, "sum3_%d" % s, [P, S])
+            acc = bank(6 + s % 2, "sum3_%d" % s, [P, S])
             nc.tensor.matmul_mx(
                 out=acc[:], lhsT=w3_q[b][0][:, cols].bitcast(FP8X4), lhsT_scale=w3_q[b][1][:, cols],
                 rhs=v2_w[:].bitcast(FP8X4), rhs_scale=v2_sc[:], start=True, stop=True,
             )
             h2 = ring.tile([P, S], F32, name="h2_%d" % s, tag="h2", bufs=3)
             nc.scalar.activation(h2[:], acc[:], ACT.Tanh)
-            nc.vector.tensor_tensor(page_b[s % 5][:].indirect(idx4[:]), h2[:], gain2[t], ALU.mult)
+            return h2[:]
 
-        place_b(0)
-        place_b(1)
+        def weigh(dst, values, gain):
+            nc.gpsimd.tensor_tensor(dst, values, gain, ALU.mult)
+            return dst
+
+        def weigh_in_place(values, gain):
+            return weigh(values, values, gain)
+
+        def place_b(s, values):
+            nc.vector.tensor_copy(page_b[s % 5][:].indirect(idx4[:]), values)
+
+        def place_a(s, values):
+            nc.vector.tensor_copy(page_a[:].indirect(idx3[:]), values)
+
+        for s in range(2):
+            nc.vector.tensor_tensor(page_b[s][:].indirect(idx4[:]), make_h2(s), gain2[s], ALU.mult)
         v_w = [gather("v_w%d" % a, U32, tab_w[a][:], idx) for a in range(2)]
         v_sc = [gather("v_sc%d" % a, U8, tab_sc[:, T * a:T * (a + 1)], idx) for a in range(2)]
-        place_b(2)
-        w1_q = {(a, 0): quantise_weight("w1_%d0" % a, w1_raw[a, 0], False) for a in range(2)}
+        place_b(2, weigh_in_place(make_h2(2), gain2[2]))
+        w1_q = {(a, 0): quantise_weight("w1_%d0" % a, w1_raw[a, 0], a == 1) for a in range(2)}
         w2_q = {0: deal_w2(0)}
+
+        def slot(k, name, shape):
+            return keep.tile(shape, F32, name=name, tag="slot%d" % (k % 3))
 
         def make_h1(s):
             b, t = divmod(s, 4)
             cols = slice(P * t, P * (t + 1))
-            acc1 = bank(0, "sum1_%d" % s, [P, S])
-            acc2 = bank(1, "sum2_%d" % s, [P, S])
+            acc1 = bank(s % 3, "sum1_%d" % s, [P, S])
+            acc2 = bank(3 + s % 3, "sum2_%d" % s, [P, S])
             for a in range(2):
                 nc.tensor.matmul_mx(
                     out=acc1[:], lhsT=w1_q[a, b][0][:, cols].bitcast(FP8X4), lhsT_scale=w1_q[a, b][1][:, cols],
@@ -219,50 +236,19 @@ def tile_list_gravimetry_storage_score_kernel(
             first = ring.tile([P, S], F32, name="first_%d" % s, tag="first")
             nc.scalar.copy(first[:], acc1[:])
             product = ring.tile([P, S], F32, name="product_%d" % s, tag="product")
-            nc.vector.tensor_tensor(product[:], acc2[:], first[:], ALU.mult)
-            h1 = ring.tile([P, S], F32, name="h1_%d" % s, tag="h1", bufs=3)
-            if s == LAST:
-                nc.scalar.activation(h1[:], product[:], ACT.Identity, bias=bias[:, s:s + 1], scale=1.0)
+            if s in PRODUCT_ON_VECTOR:
+                nc.vector.tensor_tensor(product[:], acc2[:], first[:], ALU.mult)
             else:
-                nc.scalar.activation(h1[:], product[:], ACT.Identity, bias=neg_bias[:, s:s + 1], scale=-1.0)
-            return h1
-
-        def place_a(s, h1):
-            nc.vector.tensor_tensor(page_a[s % 2][:].indirect(idx3[:]), h1[:], gain1[s % 4], ALU.mult)
-
-        turn = []
-
-        def add_transposed(name, first, second):
-            acc = bank(3 + len(turn) % 5, name, [P, 4, P])
-            turn.append(name)
-            for k in range(4):
-                nc.tensor.matmul(acc[:, k, :], first(k), ident[:], start=True, stop=False, is_transpose=True)
-                nc.tensor.matmul(acc[:, k, :], second(k), ident[:], start=False, stop=True, is_transpose=True)
-            return acc
-
-        def block(rows, h):
-            return lambda k: rows[:, HALF * h + P * k:HALF * h + P * (k + 1)]
-
-        def base_sum(s, h):
-            acc = add_transposed("base_%d_%d" % (s, h), block(page_b[s % 5], h), block(hyd_pairs[s // 2][:, s % 2, :], h))
-            base = ring.tile([P, 4, P], F32, name="base_sb_%d_%d" % (s, h), tag="base", bufs=4)
-            nc.scalar.copy(base[:], acc[:])
-            return base
-
-        def excess(s, h):
-            acc = add_transposed("diff_%d_%d" % (s, h), block(page_a[s % 2], h), block(page_b[s % 5], h))
-            over = ring.tile([P, 4, P], F32, name="over_%d_%d" % (s, h), tag="over", bufs=3)
-            nc.scalar.activation(over[:], acc[:], ACT.Relu, scale=-1.0)
-            return over
+                nc.scalar.copy(product[:], acc2[:])
+                nc.gpsimd.tensor_tensor(product[:], product[:], first[:], ALU.mult)
+            if s == 0:
+                h1 = keep.tile([P, S], F32, name="h1_0", tag="w2_sc1", align_bytes=64)
+            else:
+                h1 = slot(s - 1, "h1_%d" % s, [P, S])
+            nc.scalar.activation(h1[:], product[:], ACT.Identity, bias=bias[:, s:s + 1], scale=1.0)
+            return h1[:]
 
         planes = [held("planes%d" % b, [P, 4, M], BF16) for b in range(2)]
-
-        def finish_plane(s, h, base, over):
-            acc = add_transposed("z_%d_%d" % (s, h), lambda k: over[:, k, :], lambda k: base[:, k, :])
-            nc.scalar.activation(
-                planes[s // 4][:, s % 4, HALF * h:HALF * (h + 1)], acc[:].rearrange("p k c -> p (k c)"),
-                ACT.Copy, scale=factor[:, s:s + 1],
-            )
 
         def weave(engine_copy, woven, b, h, c0, c1):
             dst = woven[:, 4 * c0:4 * c1].rearrange("p (c i t) -> p c t i", i=4, t=4)
@@ -282,41 +268,48 @@ def tile_list_gravimetry_storage_score_kernel(
             nc.vector.quantize_mx(out=codes[:].bitcast(FP8X4), scales=scales[:], in_=woven[:])
             x_q[b, h] = (codes, scales)
 
-        h1_next = make_h1(0)
-        place_b(3)
+        ready_a = {0: weigh_in_place(make_h1(0), gain1[0])}
+        weighted_b3 = keep.tile([P, S], F32, name="weighted_b3", tag="w2_w1", align_bytes=64)
+        place_b(3, weigh(weighted_b3[:], make_h2(3), gain2[3]))
+        w3_q[1] = quantise_weight("w3_1", w3_raw[1], False)
+        ready_b = {4: weigh_in_place(make_h2(4), gain2[0])}
+        ready_a[1] = weigh(held("weighted_1", [P, S], F32)[:], make_h1(1), gain1[1])
+        ready_b[5] = weigh_in_place(make_h2(5), gain2[1])
         for s in range(LAST):
-            h1_now = h1_next
-            if s == 0:
-                w3_q[1] = quantise_weight("w3_1", w3_raw[1], False)
-            if s in (1, 2):
-                w1_q[s - 1, 1] = quantise_weight("w1_%d1" % (s - 1), w1_raw[s - 1, 1], False)
-            if s == 2:
-                w2_q[1] = deal_w2(1)
-            h1_next = make_h1(s + 1)
-            bases = [base_sum(s, h) for h in range(2)]
-            place_a(s, h1_now)
-            overs = [excess(s, h) for h in range(2)]
+            place_a(s, ready_a[s])
             if s + 4 < SLICES:
-                place_b(s + 4)
-            for h in range(2):
-                finish_plane(s, h, bases[h], overs[h])
+                place_b(s + 4, ready_b[s + 4])
+            if s < 2:
+                w1_q[s, 1] = quantise_weight("w1_%d1" % s, w1_raw[s, 1], False)
+            if s == 1:
+                w2_q[1] = deal_w2(1)
+            h1 = make_h1(s + 2) if s + 2 < SLICES else None
+            h2 = make_h2(s + 6) if s + 6 < SLICES else None
+            larger = slot(s, "larger_%d" % s, [P, M])
+            nc.vector.tensor_tensor(larger[:], page_a[:], page_b[s % 5][:], ALU.max)
+            z = hyd_pairs[s // 2][:, s % 2, :]
+            nc.gpsimd.tensor_tensor(z, larger[:], z, ALU.add)
+            if h1 is not None:
+                weighted = slot(s, "weighted_%d" % (s + 2), [P, 2, S])
+                ready_a[s + 2] = weigh(weighted[:, 0, :], h1, gain1[(s + 2) % 4])
+            if h2 is not None:
+                ready_b[s + 6] = weigh(weighted[:, 1, :], h2, gain2[(s + 6) % 4])
+            nc.scalar.activation(planes[s // 4][:, s % 4, :], z, ACT.Copy, scale=factor[:, s:s + 1])
             if s == 3:
                 quantise_x(0, 0, 0)
-                quantise_x(0, 1, HALF)
+                quantise_x(0, 1, 0)
 
         hyd_last = hyd_pairs[LAST // 2][:, LAST % 2, :]
         nc.scalar.activation(hyd_last, hyd_last, ACT.Copy, scale=factor[:, LAST:LAST + 1])
-        place_a(LAST, h1_next)
-        larger = []
+        place_a(LAST, ready_a[LAST])
+        larger = slot(LAST, "larger_%d" % LAST, [P, M])
         for h in range(2):
             cols = slice(HALF * h, HALF * (h + 1))
-            top = ring.tile([P, HALF], F32, name="larger_%d" % h, tag="over", bufs=3)
-            nc.vector.tensor_tensor(top[:], page_a[LAST % 2][:, cols], page_b[LAST % 5][:, cols], ALU.max)
-            larger.append(top)
+            nc.vector.tensor_tensor(larger[:, cols], page_a[:, cols], page_b[LAST % 5][:, cols], ALU.max)
         for h in range(2):
             cols = slice(HALF * h, HALF * (h + 1))
             nc.vector.scalar_tensor_tensor(
-                planes[1][:, 3, cols], larger[h][:], factor[:, LAST:LAST + 1], hyd_last[:, cols], ALU.mult, ALU.add,
+                planes[1][:, 3, cols], larger[:, cols], factor[:, LAST:LAST + 1], hyd_last[:, cols], ALU.mult, ALU.add,
             )
         for h in range(2):
             quantise_x(1, h, TAIL_VECTOR_COLS)

@@ -1,6 +1,7 @@
 from contextlib import ExitStack
 
 import concourse.mybir as mybir
+from concourse.masks import make_identity
 
 F32 = mybir.dt.float32
 BF16 = mybir.dt.bfloat16
@@ -20,10 +21,19 @@ T = 2048
 S = 512
 M = 1024
 HALF = 512
+QUARTER = 256
 SLICES = 8
 LAST = SLICES - 1
-TAIL_VECTOR_COLS = 320
-PRODUCT_ON_VECTOR = (0, 6, 7)
+W3_PIECES = ((0, 384), (384, 640), (640, 1024))
+W1_PIECES = ((0, 256), (256, 512), (512, 768), (768, 1024))
+LEAD = 3
+PAGES_A = 1
+HYD_AT = {0: (1,), 1: (2, 3), 2: (4, 5), 3: (6,), 4: (7,)}
+PAGE_OF = (0, 1, 2, 3, 0, 1, 2, 3)
+PLACE_B_AT = {1: 4, 2: 5, 3: 6, 4: 7}
+QUANTISE_AT = {0: ((3,), (5,)), 1: ((4,), (6,)), 2: ((5,), (7,)), 3: ((6,), ()), 4: ((7,), ())}
+TIED = (2, 3, 4, 5, 6, 7)
+SCALAR_BANKS = ()
 
 
 def tile_list_gravimetry_storage_score_kernel(
@@ -39,39 +49,42 @@ def tile_list_gravimetry_storage_score_kernel(
         def held(name, shape, dtype):
             return keep.tile(shape, dtype, name=name, align_bytes=64)
 
-        def bank(index, name, shape):
-            return psum.tile(shape, F32, name=name, tag="bank%d" % index)
+        def bank(index, name, shape, dtype=F32):
+            return psum.tile(shape, dtype, name=name, tag="bank%d" % index)
 
         tab2_sc = held("tab2_sc", [P, T], U8)
-        tab_sc = held("tab_sc", [P, 2 * T], U8)
-        w2_sc_raw = held("w2_sc_raw", [P, 2 * 1024], U8)
+        tab_sc = keep.tile([P, 2 * T], U8, name="tab_sc", tag="tab_sc", align_bytes=64)
+        w2_sc = held("w2_sc", [P, 2 * 1024], U8)
         w4_sc = held("w4_sc", [P, 2 * 512], U8)
-        page_b = [held("page_b%d" % i, [P, M], F32) for i in range(5)]
-        page_a = held("page_a", [P, M], F32)
+        vectors = held("vectors", [P, P], F32)
+        page_b = [held("page_b%d" % i, [P, M], F32) for i in range(LEAD + 1)]
+        page_a = [held("page_a%d" % i, [P, M], F32) for i in range(PAGES_A)]
         nc.gpsimd.memset(tab2_sc[:].bitcast(I32), 0)
-        nc.gpsimd.memset(tab_sc[:].bitcast(I32), 0)
-        nc.vector.memset(w2_sc_raw[:].bitcast(I32), 0)
+        nc.vector.memset(tab_sc[:].bitcast(I32), 0)
+        nc.vector.memset(w2_sc[:].bitcast(I32), 0)
+        nc.vector.memset(vectors[:], 0.0)
         nc.vector.memset(w4_sc[:].bitcast(I32), 0)
         nc.vector.memset(page_b[0][:], 0.0)
+        ident = held("ident", [P, P], F32)
+        make_identity(nc, ident[:])
+        ident_bf = held("ident_bf", [P, P], BF16)
+        make_identity(nc, ident_bf[:])
+
+        def load(name, shape, dtype, src):
+            tile = held(name, shape, dtype)
+            nc.sync.dma_start(tile[:], src)
+            return tile
 
         def load_list(name, src):
             tile = keep.tile([P, S // 16], U16, name=name)
             nc.sync.dma_start(tile[:], src)
             return tile
 
-        def stream(name, shape, src):
-            tile = ring.tile(shape, F32, name=name, tag="stream", bufs=7)
+        def load_weight(name, count, w, a, c0, c1):
+            src = w[512 * a:512 * (a + 1), c0:c1].rearrange("(p j) c -> p j c", j=4)
+            tile = ring.tile([P, 4, c1 - c0], F32, name="%s_%d_%d" % (name, a, c0), tag=name, bufs=count)
             nc.sync.dma_start(tile[:], src)
             return tile
-
-        def load_weight(name, w, a, b):
-            src = w[512 * a:512 * (a + 1), 512 * b:512 * (b + 1)].rearrange("(p j) c -> p j c", j=4)
-            return stream(name, [P, 4, 512], src)
-
-        def load_hyd(pair):
-            b, t0 = divmod(2 * pair, 4)
-            src = hyd[512 * b:512 * (b + 1), :].rearrange("(p t) m -> p t m", t=4)[:, t0:t0 + 2, :]
-            return stream("hyd%d" % pair, [P, 2, M], src)
 
         def load_words(name, src):
             tile = held(name, [P, T], U32)
@@ -84,13 +97,6 @@ def tile_list_gravimetry_storage_score_kernel(
                 dst = tile[32 * q:32 * q + 4, :].bitcast(I32).rearrange("r (a c) -> r a c", a=passes)
                 nc.sync.dma_start(dst, src[:, 4 * q:4 * q + 4, :].rearrange("a r c -> r a c").bitcast(I32))
 
-        def load_gain(name, src, t):
-            tile = held(name, [P, S], F32)
-            rows = src.rearrange("(v t) j -> v t j", t=4)[:, t, :]
-            for u in (0, 2, 1, 3):
-                nc.sync.dma_start(tile[32 * u:32 * (u + 1), :], rows)
-            return tile[:]
-
         def load_fp4_words(name, src):
             tile = held(name, [P, 2 * src.shape[2]], U8)
             nc.sync.dma_start(
@@ -99,237 +105,277 @@ def tile_list_gravimetry_storage_score_kernel(
             )
             return tile
 
-        def load_res(pair):
-            src = res[256 * pair:256 * (pair + 1), :].rearrange("(g p) m -> p g m", p=P)
-            return stream("res%d" % pair, [P, 2, M], src)
-
-        def load_rowwise(name, src):
-            tile = held(name, [P, 2, 4], F32)
-            nc.sync.dma_start(tile[:], src.rearrange("(b p t) -> p b t", b=2, t=4))
-            return tile[:].rearrange("p b t -> p (b t)")
-
-        w1_raw, w3_raw, gain1, gain2, hyd_pairs = {}, {}, {}, {}, {}
-        idx2 = load_list("idx2", offs2)
-        idx4 = load_list("idx4", offs4)
-        idx = load_list("idx", offs)
-        w3_raw[0] = load_weight("w3_raw0", w3, 0, 0)
-        tab2_w = load_words("tab2_w", tab2_words[0])
-        load_scales(tab2_sc, tab2_scales)
-        gain2[0] = load_gain("gain2_0", wg2, 0)
-        gain2[1] = load_gain("gain2_1", wg2, 1)
-        tab_w = [load_words("tab_w%d" % a, tab_words[a]) for a in range(2)]
-        load_scales(tab_sc, tab_scales)
-        gain2[2] = load_gain("gain2_2", wg2, 2)
-        w2_raw = load_fp4_words("w2_raw", w2_words)
-        load_scales(w2_sc_raw, w2_scales)
-        w1_raw[0, 0] = load_weight("w1_raw00", w1, 0, 0)
-        w1_raw[1, 0] = load_weight("w1_raw10", w1, 1, 0)
-        gain2[3] = load_gain("gain2_3", wg2, 3)
-        bias = load_rowwise("bias", b1)
-        idx3 = load_list("idx3", offs3)
-        gain1[0] = load_gain("gain1_0", wg1, 0)
-        w3_raw[1] = load_weight("w3_raw1", w3, 0, 1)
-        gain1[1] = load_gain("gain1_1", wg1, 1)
-        factor = load_rowwise("factor", cal)
-        hyd_pairs[0] = load_hyd(0)
-        gain1[2] = load_gain("gain1_2", wg1, 2)
-        w1_raw[0, 1] = load_weight("w1_raw01", w1, 0, 1)
-        gain1[3] = load_gain("gain1_3", wg1, 3)
-        w1_raw[1, 1] = load_weight("w1_raw11", w1, 1, 1)
-        hyd_pairs[1] = load_hyd(1)
-        w4_w = load_fp4_words("w4_w", w4_words)
-        load_scales(w4_sc, w4_scales)
-        hyd_pairs[2] = load_hyd(2)
-        hyd_pairs[3] = load_hyd(3)
-        res_pairs = [load_res(pair) for pair in range(2)]
-
-        def gather(name, dtype, window, offsets):
-            tile = held(name, [P, S], dtype)
-            nc.vector.tensor_copy(tile[:], window.indirect(offsets[:]))
+        def load_row_pair(name, src, pair):
+            rows = src[256 * pair:256 * (pair + 1), :].rearrange("(g p) m -> p g m", p=P)
+            tile = ring.tile([P, 2, M], F32, name="%s%d" % (name, pair), tag="rows", bufs=4)
+            nc.sync.dma_start(tile[:], rows)
             return tile
 
-        def quantise_weight(name, raw, on_vector):
-            grouped = ring.tile([P, 2048], BF16, name=name + "_bf", tag="grouped", align_bytes=64)
-            dst = grouped[:].rearrange("p (t m j) -> p m j t", t=4, j=4)
-            src = raw[:].rearrange("p j (m t) -> p m j t", t=4)
-            if on_vector:
-                nc.vector.tensor_copy(dst, src)
-            else:
-                nc.scalar.copy(dst, src)
-            codes = held(name + "_codes", [P, 512], U32)
-            scales = held(name + "_scales", [P, 512], U8)
+        w1_raw, w3_raw, hyd_pairs = {}, {}, {}
+
+        def load_w3(k):
+            w3_raw[k] = [load_weight("w3_raw", 3, w3, 0, *W3_PIECES[k])]
+
+        def load_w1(k):
+            w1_raw[k] = [load_weight("w1_raw", 8, w1, a, *W1_PIECES[k]) for a in range(2)]
+
+        idx2 = load_list("idx2", offs2)
+        load_w3(0)
+        tab2_w = load_words("tab2_w", tab2_words[0])
+        idx4 = load_list("idx4", offs4)
+        idx3 = load_list("idx3", offs3)
+        gain2 = load("gain2", [P, S], F32, wg2)
+        load_scales(tab2_sc, tab2_scales)
+        load_w3(1)
+        load_w1(0)
+        tab_w = [load_words("tab_w%d" % a, tab_words[a]) for a in range(2)]
+        load_scales(tab_sc, tab_scales)
+        load_scales(w2_sc, w2_scales)
+        w2_w = load_fp4_words("w2_w", w2_words)
+        idx = load_list("idx", offs)
+        nc.sync.dma_start(vectors[0:SLICES, :], b1.rearrange("(s p) -> s p", p=P))
+        nc.sync.dma_start(vectors[SLICES:2 * SLICES, :], cal.rearrange("(s p) -> s p", p=P))
+        load_w1(1)
+        gain1 = load("gain1", [P, S], F32, wg1)
+        load_w3(2)
+        hyd_pairs[0] = load_row_pair("hyd", hyd, 0)
+        load_w1(2)
+        hyd_pairs[1] = load_row_pair("hyd", hyd, 1)
+        load_w1(3)
+        hyd_pairs[2] = load_row_pair("hyd", hyd, 2)
+        hyd_pairs[3] = load_row_pair("hyd", hyd, 3)
+        w4_w = load_fp4_words("w4_w", w4_words)
+        load_scales(w4_sc, w4_scales)
+        res_pairs = [load_row_pair("res", res, pair) for pair in range(2)]
+
+        turned_vectors = bank(7, "turned_vectors", [P, P])
+        nc.tensor.transpose(turned_vectors[:], vectors[:], ident[:])
+        columns = held("columns", [P, 2 * SLICES], F32)
+        nc.scalar.copy(columns[:], turned_vectors[:, 0:2 * SLICES])
+        bias = columns[:, 0:SLICES]
+        factor = columns[:, SLICES:2 * SLICES]
+
+        def gather(dst, window, offsets):
+            nc.vector.tensor_copy(dst, window.indirect(offsets))
+
+        def piece(raws, pieces, s):
+            k = [c0 <= P * s < c1 for c0, c1 in pieces].index(True)
+            c0 = P * s - pieces[k][0]
+            return [raw[:, :, c0:c0 + P] for raw in raws[k]]
+
+        w1_q, w3_q = {}, {}
+
+        def quantise_weights(w1_slices, w3_slices, engine_copy, tag, bufs):
+            name = "w_%s_%s" % ("".join(map(str, w1_slices)), "".join(map(str, w3_slices)))
+            parts = [part for s in w1_slices for part in piece(w1_raw, W1_PIECES, s)]
+            parts = parts + [part for s in w3_slices for part in piece(w3_raw, W3_PIECES, s)]
+            grouped = ring.tile([P, len(parts) * 4 * P], BF16, name=name + "_bf", tag=tag, bufs=bufs, align_bytes=64)
+            for k, part in enumerate(parts):
+                dst = grouped[:, 4 * P * k:4 * P * (k + 1)].rearrange("p (c i j) -> p c j i", i=4, j=4)
+                engine_copy(dst, part.rearrange("p j (c i) -> p c j i", i=4))
+            codes = held(name + "_codes", [P, len(parts) * P], U32)
+            scales = held(name + "_scales", [P, len(parts) * P], U8)
             nc.vector.quantize_mx(out=codes[:].bitcast(FP8X4), scales=scales[:], in_=grouped[:])
-            return codes, scales
+            operands = [(codes[:, P * k:P * (k + 1)], scales[:, P * k:P * (k + 1)]) for k in range(len(parts))]
+            for k, s in enumerate(w1_slices):
+                w1_q[s] = operands[2 * k:2 * k + 2]
+            for k, s in enumerate(w3_slices):
+                w3_q[s] = operands[2 * len(w1_slices) + k]
 
-        def deal_w2(b):
-            words = keep.tile([P, 2 * 1024], U8, name="w2_w%d" % b, tag="w2_w%d" % b, align_bytes=64)
-            scales = keep.tile([P, 2 * 512], U8, name="w2_sc%d" % b, tag="w2_sc%d" % b, align_bytes=64)
-            word_src = w2_raw[:].rearrange("p (a b q t e) -> p a b t q e", a=2, b=2, t=4, e=2)
-            scale_src = w2_sc_raw[:].rearrange("p (a b q t) -> p b a t q", a=2, b=2, t=4)
-            for a in range(2):
-                nc.gpsimd.tensor_copy(
-                    words[:, 1024 * a:1024 * (a + 1)].rearrange("p (t q e) -> p t q e", t=4, e=2), word_src[:, a, b],
-                )
-            nc.gpsimd.tensor_copy(scales[:].rearrange("p (a t q) -> p a t q", a=2, t=4), scale_src[:, b])
-            return words, scales
+        v2_w = held("v2_w", [P, S], U32)
+        v2_sc = held("v2_sc", [P, S], U8)
 
-        w3_q = {0: quantise_weight("w3_0", w3_raw[0], True)}
-        v2_w = gather("v2_w", U32, tab2_w[:], idx2)
-        v2_sc = gather("v2_sc", U8, tab2_sc[:], idx2)
-
-        for page in page_b[1:] + [page_a]:
-            nc.vector.memset(page[:], 0.0)
-
-        def make_h2(s):
-            b, t = divmod(s, 4)
-            cols = slice(P * t, P * (t + 1))
-            acc = bank(6 + s % 2, "sum3_%d" % s, [P, S])
+        def make_h2(s, entries, acc_bank):
+            count = entries.stop - entries.start
+            acc = bank(acc_bank, "sum3_%d_%d" % (s, entries.start), [P, count])
+            codes, scales = w3_q[s]
             nc.tensor.matmul_mx(
-                out=acc[:], lhsT=w3_q[b][0][:, cols].bitcast(FP8X4), lhsT_scale=w3_q[b][1][:, cols],
-                rhs=v2_w[:].bitcast(FP8X4), rhs_scale=v2_sc[:], start=True, stop=True,
+                out=acc[:], lhsT=codes.bitcast(FP8X4), lhsT_scale=scales,
+                rhs=v2_w[:, entries].bitcast(FP8X4), rhs_scale=v2_sc[:, entries], start=True, stop=True,
             )
-            h2 = ring.tile([P, S], F32, name="h2_%d" % s, tag="h2", bufs=3)
+            if s == LEAD:
+                h2 = keep.tile([P, count], F32, name="h2_lead", tag="tab_sc", align_bytes=64)
+            else:
+                h2 = ring.tile([P, count], F32, name="h2_%d_%d" % (s, entries.start), tag="h2", bufs=2)
             nc.scalar.activation(h2[:], acc[:], ACT.Tanh)
-            return h2[:]
+            return h2
 
-        def weigh(dst, values, gain):
-            nc.gpsimd.tensor_tensor(dst, values, gain, ALU.mult)
-            return dst
+        def place_b(s, entries, h2):
+            offsets = idx4[:, entries.start // 16:entries.stop // 16]
+            nc.vector.tensor_tensor(page_b[PAGE_OF[s]][:].indirect(offsets), h2[:], gain2[:, entries], ALU.mult)
 
-        def weigh_in_place(values, gain):
-            return weigh(values, values, gain)
+        quantise_weights((), (0, 1, 2), nc.vector.tensor_copy, "grouped", 2)
+        for e in range(2):
+            entries = slice(256 * e, 256 * (e + 1))
+            offsets = idx2[:, 16 * e:16 * (e + 1)]
+            gather(v2_w[:, entries], tab2_w[:], offsets)
+            gather(v2_sc[:, entries], tab2_sc[:], offsets)
+        for e in range(2):
+            entries = slice(256 * e, 256 * (e + 1))
+            place_b(0, entries, make_h2(0, entries, 2 + e))
+        for page in page_b[1:] + page_a:
+            nc.vector.memset(page[:], 0.0)
+        whole = slice(0, S)
+        for s in range(1, LEAD):
+            place_b(s, whole, make_h2(s, whole, 2))
+        quantise_weights((), (3, 4), nc.scalar.copy, "grouped", 2)
+        quantise_weights((0, 1), (), nc.scalar.copy, "grouped", 2)
+        quantise_weights((2,), (), nc.scalar.copy, "grouped", 2)
 
-        def place_b(s, values):
-            nc.vector.tensor_copy(page_b[s % 5][:].indirect(idx4[:]), values)
-
-        def place_a(s, values):
-            nc.vector.tensor_copy(page_a[:].indirect(idx3[:]), values)
-
-        for s in range(2):
-            nc.vector.tensor_tensor(page_b[s][:].indirect(idx4[:]), make_h2(s), gain2[s], ALU.mult)
-        v_w = [gather("v_w%d" % a, U32, tab_w[a][:], idx) for a in range(2)]
-        v_sc = [gather("v_sc%d" % a, U8, tab_sc[:, T * a:T * (a + 1)], idx) for a in range(2)]
-        place_b(2, weigh_in_place(make_h2(2), gain2[2]))
-        w1_q = {(a, 0): quantise_weight("w1_%d0" % a, w1_raw[a, 0], a == 1) for a in range(2)}
-        w2_q = {0: deal_w2(0)}
+        v_sc = [held("v_sc%d" % a, [P, S], U8) for a in range(2)]
+        v_w = [held("v_w%d" % a, [P, S], U32) for a in range(2)]
+        for a in range(2):
+            gather(v_sc[a][:], tab_sc[:, T * a:T * (a + 1)], idx[:])
+        for a in range(2):
+            gather(v_w[a][:], tab_w[a][:], idx[:])
 
         def slot(k, name, shape):
-            return keep.tile(shape, F32, name=name, tag="slot%d" % (k % 3))
+            return keep.tile(shape, F32, name=name, tag="slot%d" % k)
+
+        def hyd_rows(s):
+            return hyd_pairs[s // 2][:, s % 2, :]
 
         def make_h1(s):
-            b, t = divmod(s, 4)
-            cols = slice(P * t, P * (t + 1))
-            acc1 = bank(s % 3, "sum1_%d" % s, [P, S])
-            acc2 = bank(3 + s % 3, "sum2_%d" % s, [P, S])
+            acc1 = bank(0, "sum1_%d" % s, [P, S])
+            acc2 = bank((1, 7)[s % 2], "sum2_%d" % s, [P, S])
             for a in range(2):
+                codes, scales = w1_q[s][a]
                 nc.tensor.matmul_mx(
-                    out=acc1[:], lhsT=w1_q[a, b][0][:, cols].bitcast(FP8X4), lhsT_scale=w1_q[a, b][1][:, cols],
+                    out=acc1[:], lhsT=codes.bitcast(FP8X4), lhsT_scale=scales,
                     rhs=v_w[a][:].bitcast(FP8X4), rhs_scale=v_sc[a][:], start=(a == 0), stop=(a == 1),
                 )
             for a in range(2):
-                c0 = 512 * a + P * t
+                c0 = 1024 * a + P * s
                 nc.tensor.matmul_mx(
-                    out=acc2[:], lhsT=w2_q[b][0][:, 2 * c0:2 * (c0 + P)].bitcast(FP4X4),
-                    lhsT_scale=w2_q[b][1][:, c0:c0 + P],
+                    out=acc2[:], lhsT=w2_w[:, 2 * c0:2 * (c0 + P)].bitcast(FP4X4), lhsT_scale=w2_sc[:, c0:c0 + P],
                     rhs=v_w[a][:].bitcast(FP8X4), rhs_scale=v_sc[a][:], start=(a == 0), stop=(a == 1),
                 )
-            first = ring.tile([P, S], F32, name="first_%d" % s, tag="first")
-            nc.scalar.copy(first[:], acc1[:])
-            product = ring.tile([P, S], F32, name="product_%d" % s, tag="product")
-            if s in PRODUCT_ON_VECTOR:
-                nc.vector.tensor_tensor(product[:], acc2[:], first[:], ALU.mult)
+            if s in TIED:
+                first = slot(0, "first_%d" % s, [P, S])[:]
             else:
-                nc.scalar.copy(product[:], acc2[:])
-                nc.gpsimd.tensor_tensor(product[:], product[:], first[:], ALU.mult)
+                first = ring.tile([P, S], F32, name="first_%d" % s, tag="first")[:]
+            nc.scalar.copy(first, acc1[:])
             if s == 0:
-                h1 = keep.tile([P, S], F32, name="h1_0", tag="w2_sc1", align_bytes=64)
+                product = held("product_0", [P, S], F32)
             else:
-                h1 = slot(s - 1, "h1_%d" % s, [P, S])
+                product = ring.tile([P, S], F32, name="product_%d" % s, tag="product", bufs=1, align_bytes=64)
+            nc.vector.tensor_tensor(product[:], acc2[:], first, ALU.mult)
+            h1 = ring.tile([P, S], F32, name="h1_%d" % s, tag="h1", bufs=2)
             nc.scalar.activation(h1[:], product[:], ACT.Identity, bias=bias[:, s:s + 1], scale=1.0)
-            return h1[:]
+            return h1
 
-        planes = [held("planes%d" % b, [P, 4, M], BF16) for b in range(2)]
+        def place_a(s, h1):
+            nc.vector.tensor_tensor(page_a[s % PAGES_A][:].indirect(idx3[:]), h1[:], gain1[:], ALU.mult)
 
-        def weave(engine_copy, woven, b, h, c0, c1):
-            dst = woven[:, 4 * c0:4 * c1].rearrange("p (c i t) -> p c t i", i=4, t=4)
-            src = planes[b][:, :, HALF * h + c0:HALF * h + c1].rearrange("p t (c i) -> p c t i", i=4)
-            engine_copy(dst, src)
+        turned = {(b, q): held("turned%d%d" % (b, q), [P, 2, 2, P, 2], BF16) for b in range(2) for q in range(4)}
+
+        def scale_rows(rows, s):
+            nc.scalar.activation(rows, rows, ACT.Copy, scale=factor[:, s:s + 1])
+
+        def turned_part(s, q):
+            part = turned[s // 4, q][:, :, :, 32 * (s % 4):32 * (s % 4 + 1), :]
+            return part.rearrange("m k u q e -> m u k q e")
+
+        def turn_sum(s, larger):
+            for h in range(2):
+                half = slice(HALF * h, HALF * (h + 1))
+                scale_rows(larger[:, half], s)
+                acc = bank(3 + h, "turned_sum_%d_%d" % (s, h), [P, 4, P])
+                for term, rows in enumerate((hyd_rows(s)[:, half], larger[:, half])):
+                    for k in range(4):
+                        nc.tensor.matmul(
+                            acc[:, k, :], rows[:, P * k:P * (k + 1)], ident[:],
+                            start=(term == 0 and k == 0), stop=(term == 1 and k == 3), is_transpose=True,
+                        )
+                for i in range(2):
+                    nc.scalar.copy(
+                        turned_part(s, 2 * h + i),
+                        acc[:, 2 * i:2 * (i + 1), :].rearrange("m k (q u e) -> m u k q e", u=2, e=2),
+                    )
 
         x_q = {}
 
-        def quantise_x(b, h, vector_cols):
-            woven = ring.tile([P, 4 * HALF], BF16, name="woven_%d_%d" % (b, h), tag="woven", align_bytes=64)
-            if vector_cols > 0:
-                weave(nc.vector.tensor_copy, woven, b, h, 0, vector_cols)
-            if vector_cols < HALF:
-                weave(nc.scalar.copy, woven, b, h, vector_cols, HALF)
-            codes = held("x_codes_%d_%d" % (b, h), [P, HALF], U32)
-            scales = held("x_scales_%d_%d" % (b, h), [P, HALF], U8)
+        def turn_back(b, q, engine_copy):
+            words = turned[b, q][:].rearrange("m k u p e -> m k u (p e)").bitcast(F32)
+            woven = ring.tile([P, 4 * QUARTER], BF16, name="woven_%d_%d" % (b, q), tag="woven", bufs=4, align_bytes=64)
+            acc = bank(5 + q % 2, "back_%d_%d" % (b, q), [P, 2, 2, P])
+            for k in range(2):
+                for u in range(2):
+                    nc.tensor.transpose(acc[:, k, u, :], words[:, k, u, :], ident[:])
+            dst = woven[:].bitcast(F32).rearrange("p (k m u) -> p k m u", k=2, u=2)
+            engine_copy(dst, acc[:].rearrange("p k u m -> p k m u"))
+            codes = held("x_codes_%d_%d" % (b, q), [P, QUARTER], U32)
+            scales = held("x_scales_%d_%d" % (b, q), [P, QUARTER], U8)
             nc.vector.quantize_mx(out=codes[:].bitcast(FP8X4), scales=scales[:], in_=woven[:])
-            x_q[b, h] = (codes, scales)
+            x_q[b, q] = (codes, scales)
 
-        ready_a = {0: weigh_in_place(make_h1(0), gain1[0])}
-        weighted_b3 = keep.tile([P, S], F32, name="weighted_b3", tag="w2_w1", align_bytes=64)
-        place_b(3, weigh(weighted_b3[:], make_h2(3), gain2[3]))
-        w3_q[1] = quantise_weight("w3_1", w3_raw[1], False)
-        ready_b = {4: weigh_in_place(make_h2(4), gain2[0])}
-        ready_a[1] = weigh(held("weighted_1", [P, S], F32)[:], make_h1(1), gain1[1])
-        ready_b[5] = weigh_in_place(make_h2(5), gain2[1])
-        for s in range(LAST):
-            place_a(s, ready_a[s])
-            if s + 4 < SLICES:
-                place_b(s + 4, ready_b[s + 4])
-            if s < 2:
-                w1_q[s, 1] = quantise_weight("w1_%d1" % s, w1_raw[s, 1], False)
-            if s == 1:
-                w2_q[1] = deal_w2(1)
-            h1 = make_h1(s + 2) if s + 2 < SLICES else None
-            h2 = make_h2(s + 6) if s + 6 < SLICES else None
-            larger = slot(s, "larger_%d" % s, [P, M])
-            nc.vector.tensor_tensor(larger[:], page_a[:], page_b[s % 5][:], ALU.max)
-            z = hyd_pairs[s // 2][:, s % 2, :]
-            nc.gpsimd.tensor_tensor(z, larger[:], z, ALU.add)
-            if h1 is not None:
-                weighted = slot(s, "weighted_%d" % (s + 2), [P, 2, S])
-                ready_a[s + 2] = weigh(weighted[:, 0, :], h1, gain1[(s + 2) % 4])
-            if h2 is not None:
-                ready_b[s + 6] = weigh(weighted[:, 1, :], h2, gain2[(s + 6) % 4])
-            nc.scalar.activation(planes[s // 4][:, s % 4, :], z, ACT.Copy, scale=factor[:, s:s + 1])
+        h2 = {LEAD: make_h2(LEAD, whole, 2)}
+        place_b(LEAD, whole, h2[LEAD])
+        h1 = {s: make_h1(s) for s in range(2)}
+        scale_rows(hyd_rows(0), 0)
+        for s in range(SLICES):
+            place_a(s, h1[s])
+            if s in PLACE_B_AT:
+                place_b(PLACE_B_AT[s], whole, h2[PLACE_B_AT[s]])
+            if s in QUANTISE_AT:
+                quantise_weights(*QUANTISE_AT[s], nc.scalar.copy, *(("grouped", 2) if s == 0 else ("product", 1)))
+            if s + 2 < SLICES:
+                h1[s + 2] = make_h1(s + 2)
+            if s + LEAD + 1 < SLICES:
+                h2[s + LEAD + 1] = make_h2(s + LEAD + 1, whole, 0)
+            if s < LAST:
+                larger = slot(0, "larger_%d" % s, [P, M])
+                nc.vector.tensor_tensor(larger[:], page_a[s % PAGES_A][:], page_b[PAGE_OF[s]][:], ALU.max)
+                turn_sum(s, larger)
+            for ahead in HYD_AT.get(s, ()):
+                scale_rows(hyd_rows(ahead), ahead)
             if s == 3:
-                quantise_x(0, 0, 0)
-                quantise_x(0, 1, 0)
+                for q in range(4):
+                    turn_back(0, q, nc.scalar.copy)
 
-        hyd_last = hyd_pairs[LAST // 2][:, LAST % 2, :]
-        nc.scalar.activation(hyd_last, hyd_last, ACT.Copy, scale=factor[:, LAST:LAST + 1])
-        place_a(LAST, ready_a[LAST])
-        larger = slot(LAST, "larger_%d" % LAST, [P, M])
-        for h in range(2):
-            cols = slice(HALF * h, HALF * (h + 1))
-            nc.vector.tensor_tensor(larger[:, cols], page_a[:, cols], page_b[LAST % 5][:, cols], ALU.max)
-        for h in range(2):
-            cols = slice(HALF * h, HALF * (h + 1))
-            nc.vector.scalar_tensor_tensor(
-                planes[1][:, 3, cols], larger[:, cols], factor[:, LAST:LAST + 1], hyd_last[:, cols], ALU.mult, ALU.add,
+        larger = slot(0, "larger_last", [P, M])
+        x_last = held("x_last", [P, M], BF16)
+        quarters = [slice(QUARTER * q, QUARTER * (q + 1)) for q in range(4)]
+        for pair in (quarters[:2], quarters[2:]):
+            for cols in pair:
+                nc.vector.tensor_tensor(
+                    larger[:, cols], page_a[LAST % PAGES_A][:, cols], page_b[PAGE_OF[LAST]][:, cols], ALU.max,
+                )
+            for cols in pair:
+                nc.vector.scalar_tensor_tensor(
+                    x_last[:, cols], larger[:, cols], factor[:, LAST:LAST + 1], hyd_rows(LAST)[:, cols], ALU.mult, ALU.add,
+                )
+        for q in range(4):
+            acc = bank(3 + q % 2, "turned_last_%d" % q, [P, 2, P], BF16)
+            for k in range(2):
+                nc.tensor.transpose(acc[:, k, :], x_last[:, QUARTER * q + P * k:QUARTER * q + P * (k + 1)], ident_bf[:])
+            nc.scalar.copy(
+                turned_part(LAST, q).bitcast(F32),
+                acc[:].bitcast(F32).rearrange("m k (q u e) -> m u k q e", u=2, e=1),
             )
-        for h in range(2):
-            quantise_x(1, h, TAIL_VECTOR_COLS)
+        for q in range(4):
+            turn_back(1, q, nc.scalar.copy)
 
-        sums = {}
-        for b in range(2):
-            for h in range(2):
+        out_banks = ((0, 1), (2, 7), (3, 4), (5, 6))
+        for q in range(4):
+            sums = [bank(out_banks[q][pair], "out_%d_%d" % (q, pair), [P, 2, QUARTER]) for pair in range(2)]
+            for b in range(2):
+                codes, scales = x_q[b, q]
                 for g in range(4):
-                    if b == 0:
-                        sums[h, g] = bank(4 * h + g, "out_%d_%d" % (h, g), [P, HALF])
                     c0 = 512 * b + P * g
                     nc.tensor.matmul_mx(
-                        out=sums[h, g][:], lhsT=w4_w[:, 2 * c0:2 * (c0 + P)].bitcast(FP4X4),
-                        lhsT_scale=w4_sc[:, c0:c0 + P],
-                        rhs=x_q[b, h][0][:].bitcast(FP8X4), rhs_scale=x_q[b, h][1][:],
-                        start=(b == 0), stop=(b == 1),
+                        out=sums[g // 2][:, g % 2, :], lhsT=w4_w[:, 2 * c0:2 * (c0 + P)].bitcast(FP4X4),
+                        lhsT_scale=w4_sc[:, c0:c0 + P], rhs=codes[:].bitcast(FP8X4), rhs_scale=scales[:],
+                        start=(b == 0 and g % 2 == 0), stop=(b == 1 and g % 2 == 1),
                     )
-        for h in range(2):
-            cols = slice(HALF * h, HALF * (h + 1))
-            for g in range(4):
-                rows = res_pairs[g // 2][:, g % 2, cols]
-                nc.vector.tensor_tensor(rows, sums[h, g][:], rows, ALU.add)
-                nc.sync.dma_start(out[P * g:P * (g + 1), cols], rows)
+            for pair in range(2):
+                rows = res_pairs[pair][:, :, quarters[q]]
+                result = ring.tile([P, 2, QUARTER], F32, name="result_%d_%d" % (q, pair), tag="w1_raw", bufs=8)
+                if (q, pair) in SCALAR_BANKS:
+                    staged = ring.tile([P, 2, QUARTER], F32, name="staged_%d_%d" % (q, pair), tag="first")
+                    nc.scalar.copy(staged[:], sums[pair][:])
+                    nc.gpsimd.tensor_tensor(result[:], staged[:], rows, ALU.add)
+                else:
+                    nc.vector.tensor_tensor(result[:], sums[pair][:], rows, ALU.add)
+                dst = out[256 * pair:256 * (pair + 1), quarters[q]].rearrange("(g p) m -> p g m", p=P)
+                nc.sync.dma_start(dst, result[:])

@@ -24,7 +24,7 @@ HALF = 512
 QUARTER = 256
 SLICES = 8
 LAST = SLICES - 1
-W3_PIECES = ((0, 384), (384, 640), (640, 1024))
+W3_PIECES = ((0, 128), (128, 384), (384, 640), (640, 1024))
 W1_PIECES = ((0, 256), (256, 512), (512, 768), (768, 1024))
 LEAD = 3
 PAGES_A = 1
@@ -32,6 +32,8 @@ HYD_AT = {0: (1,), 1: (2, 3), 2: (4, 5), 3: (6,), 4: (7,)}
 PAGE_OF = (0, 1, 2, 3, 0, 1, 2, 3)
 PLACE_B_AT = {1: 4, 2: 5, 3: 6, 4: 7}
 QUANTISE_AT = {0: ((3,), (5,)), 1: ((4,), (6,)), 2: ((5,), (7,)), 3: ((6,), ()), 4: ((7,), ())}
+SUM1_BANKS = (0, 1, 1, 0, 0, 0, 0, 0)
+SUM2_BANKS = (1, 7, 2, 1, 7, 1, 7, 1)
 TIED = (2, 3, 4, 5, 6, 7)
 SCALAR_BANKS = ()
 
@@ -64,7 +66,8 @@ def tile_list_gravimetry_storage_score_kernel(
         nc.vector.memset(w2_sc[:].bitcast(I32), 0)
         nc.vector.memset(vectors[:], 0.0)
         nc.vector.memset(w4_sc[:].bitcast(I32), 0)
-        nc.vector.memset(page_b[0][:], 0.0)
+        for page in page_b + page_a:
+            nc.vector.memset(page[:], 0.0)
         ident = held("ident", [P, P], F32)
         make_identity(nc, ident[:])
         ident_bf = held("ident_bf", [P, P], BF16)
@@ -114,30 +117,31 @@ def tile_list_gravimetry_storage_score_kernel(
         w1_raw, w3_raw, hyd_pairs = {}, {}, {}
 
         def load_w3(k):
-            w3_raw[k] = [load_weight("w3_raw", 3, w3, 0, *W3_PIECES[k])]
+            w3_raw[k] = [load_weight("w3_raw%d" % k, 1, w3, 0, *W3_PIECES[k])]
 
         def load_w1(k):
             w1_raw[k] = [load_weight("w1_raw", 8, w1, a, *W1_PIECES[k]) for a in range(2)]
 
         idx2 = load_list("idx2", offs2)
-        load_w3(0)
         tab2_w = load_words("tab2_w", tab2_words[0])
+        load_w3(0)
+        load_w3(1)
         idx4 = load_list("idx4", offs4)
         idx3 = load_list("idx3", offs3)
-        gain2 = load("gain2", [P, S], F32, wg2)
         load_scales(tab2_sc, tab2_scales)
-        load_w3(1)
+        gain2 = load("gain2", [P, S], F32, wg2)
+        load_w3(2)
         load_w1(0)
-        tab_w = [load_words("tab_w%d" % a, tab_words[a]) for a in range(2)]
-        load_scales(tab_sc, tab_scales)
-        load_scales(w2_sc, w2_scales)
-        w2_w = load_fp4_words("w2_w", w2_words)
-        idx = load_list("idx", offs)
         nc.sync.dma_start(vectors[0:SLICES, :], b1.rearrange("(s p) -> s p", p=P))
         nc.sync.dma_start(vectors[SLICES:2 * SLICES, :], cal.rearrange("(s p) -> s p", p=P))
+        tab_w = [load_words("tab_w%d" % a, tab_words[a]) for a in range(2)]
+        load_scales(tab_sc, tab_scales)
+        idx = load_list("idx", offs)
         load_w1(1)
+        load_scales(w2_sc, w2_scales)
+        w2_w = load_fp4_words("w2_w", w2_words)
         gain1 = load("gain1", [P, S], F32, wg1)
-        load_w3(2)
+        load_w3(3)
         hyd_pairs[0] = load_row_pair("hyd", hyd, 0)
         load_w1(2)
         hyd_pairs[1] = load_row_pair("hyd", hyd, 1)
@@ -204,17 +208,14 @@ def tile_list_gravimetry_storage_score_kernel(
             offsets = idx4[:, entries.start // 16:entries.stop // 16]
             nc.vector.tensor_tensor(page_b[PAGE_OF[s]][:].indirect(offsets), h2[:], gain2[:, entries], ALU.mult)
 
+        list_halves = [slice(256 * e, 256 * (e + 1)) for e in range(2)]
+        for e, entries in enumerate(list_halves):
+            gather(v2_w[:, entries], tab2_w[:], idx2[:, 16 * e:16 * (e + 1)])
         quantise_weights((), (0, 1, 2), nc.vector.tensor_copy, "grouped", 2)
-        for e in range(2):
-            entries = slice(256 * e, 256 * (e + 1))
-            offsets = idx2[:, 16 * e:16 * (e + 1)]
-            gather(v2_w[:, entries], tab2_w[:], offsets)
-            gather(v2_sc[:, entries], tab2_sc[:], offsets)
-        for e in range(2):
-            entries = slice(256 * e, 256 * (e + 1))
+        for e, entries in enumerate(list_halves):
+            gather(v2_sc[:, entries], tab2_sc[:], idx2[:, 16 * e:16 * (e + 1)])
+        for e, entries in enumerate(list_halves):
             place_b(0, entries, make_h2(0, entries, 2 + e))
-        for page in page_b[1:] + page_a:
-            nc.vector.memset(page[:], 0.0)
         whole = slice(0, S)
         for s in range(1, LEAD):
             place_b(s, whole, make_h2(s, whole, 2))
@@ -236,8 +237,8 @@ def tile_list_gravimetry_storage_score_kernel(
             return hyd_pairs[s // 2][:, s % 2, :]
 
         def make_h1(s):
-            acc1 = bank(0, "sum1_%d" % s, [P, S])
-            acc2 = bank((1, 7)[s % 2], "sum2_%d" % s, [P, S])
+            acc1 = bank(SUM1_BANKS[s], "sum1_%d" % s, [P, S])
+            acc2 = bank(SUM2_BANKS[s], "sum2_%d" % s, [P, S])
             for a in range(2):
                 codes, scales = w1_q[s][a]
                 nc.tensor.matmul_mx(
@@ -255,10 +256,10 @@ def tile_list_gravimetry_storage_score_kernel(
             else:
                 first = ring.tile([P, S], F32, name="first_%d" % s, tag="first")[:]
             nc.scalar.copy(first, acc1[:])
-            if s == 0:
-                product = held("product_0", [P, S], F32)
+            if s < 1:
+                product = held("product_%d" % s, [P, S], F32)
             else:
-                product = ring.tile([P, S], F32, name="product_%d" % s, tag="product", bufs=1, align_bytes=64)
+                product = ring.tile([P, S], F32, name="product_%d" % s, tag="product", bufs=2, align_bytes=64)
             nc.vector.tensor_tensor(product[:], acc2[:], first, ALU.mult)
             h1 = ring.tile([P, S], F32, name="h1_%d" % s, tag="h1", bufs=2)
             nc.scalar.activation(h1[:], product[:], ACT.Identity, bias=bias[:, s:s + 1], scale=1.0)
@@ -295,10 +296,10 @@ def tile_list_gravimetry_storage_score_kernel(
 
         x_q = {}
 
-        def turn_back(b, q, engine_copy):
+        def turn_back(b, q, acc_bank, engine_copy):
             words = turned[b, q][:].rearrange("m k u p e -> m k u (p e)").bitcast(F32)
             woven = ring.tile([P, 4 * QUARTER], BF16, name="woven_%d_%d" % (b, q), tag="woven", bufs=4, align_bytes=64)
-            acc = bank(5 + q % 2, "back_%d_%d" % (b, q), [P, 2, 2, P])
+            acc = bank(acc_bank, "back_%d_%d" % (b, q), [P, 2, 2, P])
             for k in range(2):
                 for u in range(2):
                     nc.tensor.transpose(acc[:, k, u, :], words[:, k, u, :], ident[:])
@@ -318,7 +319,7 @@ def tile_list_gravimetry_storage_score_kernel(
             if s in PLACE_B_AT:
                 place_b(PLACE_B_AT[s], whole, h2[PLACE_B_AT[s]])
             if s in QUANTISE_AT:
-                quantise_weights(*QUANTISE_AT[s], nc.scalar.copy, *(("grouped", 2) if s == 0 else ("product", 1)))
+                quantise_weights(*QUANTISE_AT[s], nc.scalar.copy, *(("grouped", 2) if s == 0 else ("product", 2)))
             if s + 2 < SLICES:
                 h1[s + 2] = make_h1(s + 2)
             if s + LEAD + 1 < SLICES:
@@ -331,7 +332,7 @@ def tile_list_gravimetry_storage_score_kernel(
                 scale_rows(hyd_rows(ahead), ahead)
             if s == 3:
                 for q in range(4):
-                    turn_back(0, q, nc.scalar.copy)
+                    turn_back(0, q, 5 + q % 2, nc.scalar.copy)
 
         larger = slot(0, "larger_last", [P, M])
         x_last = held("x_last", [P, M], BF16)
@@ -346,7 +347,7 @@ def tile_list_gravimetry_storage_score_kernel(
                     x_last[:, cols], larger[:, cols], factor[:, LAST:LAST + 1], hyd_rows(LAST)[:, cols], ALU.mult, ALU.add,
                 )
         for q in range(4):
-            acc = bank(3 + q % 2, "turned_last_%d" % q, [P, 2, P], BF16)
+            acc = bank((3, 4, 3, 4)[q], "turned_last_%d" % q, [P, 2, P], BF16)
             for k in range(2):
                 nc.tensor.transpose(acc[:, k, :], x_last[:, QUARTER * q + P * k:QUARTER * q + P * (k + 1)], ident_bf[:])
             nc.scalar.copy(
@@ -354,7 +355,7 @@ def tile_list_gravimetry_storage_score_kernel(
                 acc[:].bitcast(F32).rearrange("m k (q u e) -> m u k q e", u=2, e=1),
             )
         for q in range(4):
-            turn_back(1, q, nc.scalar.copy)
+            turn_back(1, q, (5, 6, 5, 6)[q], nc.scalar.copy)
 
         out_banks = ((0, 1), (2, 7), (3, 4), (5, 6))
         for q in range(4):

@@ -20,22 +20,20 @@ P = 128
 T = 2048
 S = 512
 M = 1024
-HALF = 512
-QUARTER = 256
-SLICES = 8
+K_PASS = 512
+H = 1024
+N = 512
+HALF = M // 2
+QUARTER = M // 4
+SLICES = H // P
 LAST = SLICES - 1
+SLICES_A_PASS = K_PASS // P
 W3_PIECES = ((0, 128), (128, 384), (384, 640), (640, 1024))
 W1_PIECES = ((0, 256), (256, 512), (512, 768), (768, 1024))
 LEAD = 3
-PAGES_A = 1
-HYD_AT = {0: (1,), 1: (2, 3), 2: (4, 5), 3: (6,), 4: (7,)}
-PAGE_OF = (0, 1, 2, 3, 0, 1, 2, 3)
-PLACE_B_AT = {1: 4, 2: 5, 3: 6, 4: 7}
-QUANTISE_AT = {0: ((3,), (5,)), 1: ((4,), (6,)), 2: ((5,), (7,)), 3: ((6,), ()), 4: ((7,), ())}
-SUM1_BANKS = (0, 1, 1, 0, 0, 0, 0, 0)
-SUM2_BANKS = (1, 7, 2, 1, 7, 1, 7, 1)
-TIED = (2, 3, 4, 5, 6, 7)
-SCALAR_BANKS = ()
+PB_PAGES = LEAD + 1
+W1_BUFS = 7
+ROW_BUFS = 4
 
 
 def tile_list_gravimetry_storage_score_kernel(
@@ -48,33 +46,33 @@ def tile_list_gravimetry_storage_score_kernel(
         ring = ctx.enter_context(tc.tile_pool(name="ring", bufs=2))
         psum = ctx.enter_context(tc.psum_pool(name="psum", bufs=1))
 
-        def held(name, shape, dtype):
-            return keep.tile(shape, dtype, name=name, align_bytes=64)
+        def held(name, shape, dtype, buffer=None):
+            return keep.tile(shape, dtype, name=name, tag=buffer or name, align_bytes=64)
 
         def bank(index, name, shape, dtype=F32):
             return psum.tile(shape, dtype, name=name, tag="bank%d" % index)
 
         tab2_sc = held("tab2_sc", [P, T], U8)
-        tab_sc = keep.tile([P, 2 * T], U8, name="tab_sc", tag="tab_sc", align_bytes=64)
-        w2_sc = held("w2_sc", [P, 2 * 1024], U8)
-        w4_sc = held("w4_sc", [P, 2 * 512], U8)
-        vectors = held("vectors", [P, P], F32)
-        page_b = [held("page_b%d" % i, [P, M], F32) for i in range(LEAD + 1)]
-        page_a = [held("page_a%d" % i, [P, M], F32) for i in range(PAGES_A)]
+        tab_sc = held("tab_sc", [P, 2 * T], U8)
+        w2_sc = held("w2_sc", [P, 2 * H], U8)
+        w4_sc = held("w4_sc", [P, 2 * N], U8)
+        vector_rows = held("vector_rows", [P, P], F32)
+        pages_b = [held("page_b%d" % i, [P, M], F32) for i in range(PB_PAGES)]
+        page_a = held("page_a", [P, M], F32)
         nc.gpsimd.memset(tab2_sc[:].bitcast(I32), 0)
         nc.vector.memset(tab_sc[:].bitcast(I32), 0)
         nc.vector.memset(w2_sc[:].bitcast(I32), 0)
-        nc.vector.memset(vectors[:], 0.0)
+        nc.vector.memset(vector_rows[:], 0.0)
         nc.vector.memset(w4_sc[:].bitcast(I32), 0)
-        for page in page_b + page_a:
+        for page in pages_b + [page_a]:
             nc.vector.memset(page[:], 0.0)
         ident = held("ident", [P, P], F32)
         make_identity(nc, ident[:])
         ident_bf = held("ident_bf", [P, P], BF16)
         make_identity(nc, ident_bf[:])
 
-        def load(name, shape, dtype, src):
-            tile = held(name, shape, dtype)
+        def load_gain(name, src):
+            tile = held(name, [P, S], F32)
             nc.sync.dma_start(tile[:], src)
             return tile
 
@@ -83,13 +81,13 @@ def tile_list_gravimetry_storage_score_kernel(
             nc.sync.dma_start(tile[:], src)
             return tile
 
-        def load_weight(name, count, w, a, c0, c1):
-            src = w[512 * a:512 * (a + 1), c0:c1].rearrange("(p j) c -> p j c", j=4)
-            tile = ring.tile([P, 4, c1 - c0], F32, name="%s_%d_%d" % (name, a, c0), tag=name, bufs=count)
+        def load_weight(tag, bufs, w, a, c0, c1):
+            src = w[K_PASS * a:K_PASS * (a + 1), c0:c1].rearrange("(p j) c -> p j c", j=4)
+            tile = ring.tile([P, 4, c1 - c0], F32, name="%s_%d_%d" % (tag, a, c0), tag=tag, bufs=bufs)
             nc.sync.dma_start(tile[:], src)
             return tile
 
-        def load_words(name, src):
+        def load_table_words(name, src):
             tile = held(name, [P, T], U32)
             nc.sync.dma_start(tile[:].bitcast(I32), src.rearrange("p c i -> p (c i)").bitcast(I32))
             return tile
@@ -109,8 +107,8 @@ def tile_list_gravimetry_storage_score_kernel(
             return tile
 
         def load_row_pair(name, src, pair):
-            rows = src[256 * pair:256 * (pair + 1), :].rearrange("(g p) m -> p g m", p=P)
-            tile = ring.tile([P, 2, M], F32, name="%s%d" % (name, pair), tag="rows", bufs=4)
+            rows = src[2 * P * pair:2 * P * (pair + 1), :].rearrange("(g p) m -> p g m", p=P)
+            tile = ring.tile([P, 2, M], F32, name="%s%d" % (name, pair), tag="rows", bufs=ROW_BUFS)
             nc.sync.dma_start(tile[:], rows)
             return tile
 
@@ -120,27 +118,27 @@ def tile_list_gravimetry_storage_score_kernel(
             w3_raw[k] = [load_weight("w3_raw%d" % k, 1, w3, 0, *W3_PIECES[k])]
 
         def load_w1(k):
-            w1_raw[k] = [load_weight("w1_raw", 8, w1, a, *W1_PIECES[k]) for a in range(2)]
+            w1_raw[k] = [load_weight("w1_raw", W1_BUFS, w1, a, *W1_PIECES[k]) for a in range(2)]
 
         idx2 = load_list("idx2", offs2)
-        tab2_w = load_words("tab2_w", tab2_words[0])
+        tab2_w = load_table_words("tab2_w", tab2_words[0])
         load_w3(0)
         load_w3(1)
         idx4 = load_list("idx4", offs4)
         idx3 = load_list("idx3", offs3)
         load_scales(tab2_sc, tab2_scales)
-        gain2 = load("gain2", [P, S], F32, wg2)
+        gain2 = load_gain("gain2", wg2)
         load_w3(2)
         load_w1(0)
-        nc.sync.dma_start(vectors[0:SLICES, :], b1.rearrange("(s p) -> s p", p=P))
-        nc.sync.dma_start(vectors[SLICES:2 * SLICES, :], cal.rearrange("(s p) -> s p", p=P))
-        tab_w = [load_words("tab_w%d" % a, tab_words[a]) for a in range(2)]
+        nc.sync.dma_start(vector_rows[0:SLICES, :], b1.rearrange("(s p) -> s p", p=P))
+        nc.sync.dma_start(vector_rows[SLICES:2 * SLICES, :], cal.rearrange("(s p) -> s p", p=P))
+        tab_w = [load_table_words("tab_w%d" % a, tab_words[a]) for a in range(2)]
         load_scales(tab_sc, tab_scales)
         idx = load_list("idx", offs)
         load_w1(1)
         load_scales(w2_sc, w2_scales)
         w2_w = load_fp4_words("w2_w", w2_words)
-        gain1 = load("gain1", [P, S], F32, wg1)
+        gain1 = load_gain("gain1", wg1)
         load_w3(3)
         hyd_pairs[0] = load_row_pair("hyd", hyd, 0)
         load_w1(2)
@@ -153,31 +151,31 @@ def tile_list_gravimetry_storage_score_kernel(
         res_pairs = [load_row_pair("res", res, pair) for pair in range(2)]
 
         turned_vectors = bank(7, "turned_vectors", [P, P])
-        nc.tensor.transpose(turned_vectors[:], vectors[:], ident[:])
-        columns = held("columns", [P, 2 * SLICES], F32)
-        nc.scalar.copy(columns[:], turned_vectors[:, 0:2 * SLICES])
-        bias = columns[:, 0:SLICES]
-        factor = columns[:, SLICES:2 * SLICES]
+        nc.tensor.transpose(turned_vectors[:], vector_rows[:], ident[:])
+        vector_columns = held("vector_columns", [P, 2 * SLICES], F32)
+        nc.scalar.copy(vector_columns[:], turned_vectors[:, 0:2 * SLICES])
+        bias = vector_columns[:, 0:SLICES]
+        factor = vector_columns[:, SLICES:2 * SLICES]
 
         def gather(dst, window, offsets):
             nc.vector.tensor_copy(dst, window.indirect(offsets))
 
-        def piece(raws, pieces, s):
+        def slice_columns(raws, pieces, s):
             k = [c0 <= P * s < c1 for c0, c1 in pieces].index(True)
             c0 = P * s - pieces[k][0]
             return [raw[:, :, c0:c0 + P] for raw in raws[k]]
 
         w1_q, w3_q = {}, {}
 
-        def quantise_weights(w1_slices, w3_slices, engine_copy, tag, bufs):
+        def quantise_weights(w1_slices, w3_slices, engine_copy, tag, codes_buffer=None):
             name = "w_%s_%s" % ("".join(map(str, w1_slices)), "".join(map(str, w3_slices)))
-            parts = [part for s in w1_slices for part in piece(w1_raw, W1_PIECES, s)]
-            parts = parts + [part for s in w3_slices for part in piece(w3_raw, W3_PIECES, s)]
-            grouped = ring.tile([P, len(parts) * 4 * P], BF16, name=name + "_bf", tag=tag, bufs=bufs, align_bytes=64)
+            parts = [part for s in w1_slices for part in slice_columns(w1_raw, W1_PIECES, s)]
+            parts = parts + [part for s in w3_slices for part in slice_columns(w3_raw, W3_PIECES, s)]
+            grouped = ring.tile([P, len(parts) * 4 * P], BF16, name=name + "_bf", tag=tag, align_bytes=64)
             for k, part in enumerate(parts):
                 dst = grouped[:, 4 * P * k:4 * P * (k + 1)].rearrange("p (c i j) -> p c j i", i=4, j=4)
                 engine_copy(dst, part.rearrange("p j (c i) -> p c j i", i=4))
-            codes = held(name + "_codes", [P, len(parts) * P], U32)
+            codes = held(name + "_codes", [P, len(parts) * P], U32, codes_buffer)
             scales = held(name + "_scales", [P, len(parts) * P], U8)
             nc.vector.quantize_mx(out=codes[:].bitcast(FP8X4), scales=scales[:], in_=grouped[:])
             operands = [(codes[:, P * k:P * (k + 1)], scales[:, P * k:P * (k + 1)]) for k in range(len(parts))]
@@ -198,30 +196,29 @@ def tile_list_gravimetry_storage_score_kernel(
                 rhs=v2_w[:, entries].bitcast(FP8X4), rhs_scale=v2_sc[:, entries], start=True, stop=True,
             )
             if s == LEAD:
-                h2 = keep.tile([P, count], F32, name="h2_lead", tag="tab_sc", align_bytes=64)
+                h2 = held("h2_lead", [P, count], F32, "tab_sc")
             else:
-                h2 = ring.tile([P, count], F32, name="h2_%d_%d" % (s, entries.start), tag="h2", bufs=2)
+                h2 = ring.tile([P, count], F32, name="h2_%d_%d" % (s, entries.start), tag="h2")
             nc.scalar.activation(h2[:], acc[:], ACT.Tanh)
             return h2
 
         def place_b(s, entries, h2):
             offsets = idx4[:, entries.start // 16:entries.stop // 16]
-            nc.vector.tensor_tensor(page_b[PAGE_OF[s]][:].indirect(offsets), h2[:], gain2[:, entries], ALU.mult)
+            nc.vector.tensor_tensor(pages_b[s % PB_PAGES][:].indirect(offsets), h2[:], gain2[:, entries], ALU.mult)
 
-        list_halves = [slice(256 * e, 256 * (e + 1)) for e in range(2)]
-        for e, entries in enumerate(list_halves):
-            gather(v2_w[:, entries], tab2_w[:], idx2[:, 16 * e:16 * (e + 1)])
-        quantise_weights((), (0, 1, 2), nc.vector.tensor_copy, "grouped", 2)
-        for e, entries in enumerate(list_halves):
-            gather(v2_sc[:, entries], tab2_sc[:], idx2[:, 16 * e:16 * (e + 1)])
+        list_halves = [slice(S // 2 * e, S // 2 * (e + 1)) for e in range(2)]
+        for entries in list_halves:
+            gather(v2_w[:, entries], tab2_w[:], idx2[:, entries.start // 16:entries.stop // 16])
+        quantise_weights((), range(LEAD), nc.vector.tensor_copy, "grouped")
+        for entries in list_halves:
+            gather(v2_sc[:, entries], tab2_sc[:], idx2[:, entries.start // 16:entries.stop // 16])
         for e, entries in enumerate(list_halves):
             place_b(0, entries, make_h2(0, entries, 2 + e))
         whole = slice(0, S)
         for s in range(1, LEAD):
             place_b(s, whole, make_h2(s, whole, 2))
-        quantise_weights((), (3, 4), nc.scalar.copy, "grouped", 2)
-        quantise_weights((0, 1), (), nc.scalar.copy, "grouped", 2)
-        quantise_weights((2,), (), nc.scalar.copy, "grouped", 2)
+        quantise_weights((), (LEAD, LEAD + 1), nc.scalar.copy, "grouped")
+        quantise_weights((0, 1), (), nc.scalar.copy, "grouped")
 
         v_sc = [held("v_sc%d" % a, [P, S], U8) for a in range(2)]
         v_w = [held("v_w%d" % a, [P, S], U32) for a in range(2)]
@@ -230,15 +227,9 @@ def tile_list_gravimetry_storage_score_kernel(
         for a in range(2):
             gather(v_w[a][:], tab_w[a][:], idx[:])
 
-        def slot(k, name, shape):
-            return keep.tile(shape, F32, name=name, tag="slot%d" % k)
-
-        def hyd_rows(s):
-            return hyd_pairs[s // 2][:, s % 2, :]
-
-        def make_h1(s):
-            acc1 = bank(SUM1_BANKS[s], "sum1_%d" % s, [P, S])
-            acc2 = bank(SUM2_BANKS[s], "sum2_%d" % s, [P, S])
+        def make_sums(s):
+            acc1 = bank(1 if s in (1, 2) else 0, "sum1_%d" % s, [P, S])
+            acc2 = bank({0: 1, 1: 7, 2: 2}.get(s, (7, 1)[s % 2]), "sum2_%d" % s, [P, S])
             for a in range(2):
                 codes, scales = w1_q[s][a]
                 nc.tensor.matmul_mx(
@@ -246,137 +237,156 @@ def tile_list_gravimetry_storage_score_kernel(
                     rhs=v_w[a][:].bitcast(FP8X4), rhs_scale=v_sc[a][:], start=(a == 0), stop=(a == 1),
                 )
             for a in range(2):
-                c0 = 1024 * a + P * s
+                c0 = H * a + P * s
                 nc.tensor.matmul_mx(
                     out=acc2[:], lhsT=w2_w[:, 2 * c0:2 * (c0 + P)].bitcast(FP4X4), lhsT_scale=w2_sc[:, c0:c0 + P],
                     rhs=v_w[a][:].bitcast(FP8X4), rhs_scale=v_sc[a][:], start=(a == 0), stop=(a == 1),
                 )
-            if s in TIED:
-                first = slot(0, "first_%d" % s, [P, S])[:]
+            sum1 = held("sum1_sb_%d" % s, [P, S], F32, "step" if s >= 2 else None)
+            nc.scalar.copy(sum1[:], acc1[:])
+            return sum1, acc2
+
+        def make_h1(s, sum1, acc2):
+            if s == 0:
+                product = held("product_0", [P, S], F32)
             else:
-                first = ring.tile([P, S], F32, name="first_%d" % s, tag="first")[:]
-            nc.scalar.copy(first, acc1[:])
-            if s < 1:
-                product = held("product_%d" % s, [P, S], F32)
-            else:
-                product = ring.tile([P, S], F32, name="product_%d" % s, tag="product", bufs=2, align_bytes=64)
-            nc.vector.tensor_tensor(product[:], acc2[:], first, ALU.mult)
-            h1 = ring.tile([P, S], F32, name="h1_%d" % s, tag="h1", bufs=2)
+                product = ring.tile([P, S], F32, name="product_%d" % s, tag="product", align_bytes=64)
+            nc.vector.tensor_tensor(product[:], acc2[:], sum1[:], ALU.mult)
+            h1 = ring.tile([P, S], F32, name="h1_%d" % s, tag="h1")
             nc.scalar.activation(h1[:], product[:], ACT.Identity, bias=bias[:, s:s + 1], scale=1.0)
             return h1
 
         def place_a(s, h1):
-            nc.vector.tensor_tensor(page_a[s % PAGES_A][:].indirect(idx3[:]), h1[:], gain1[:], ALU.mult)
+            nc.vector.tensor_tensor(page_a[:].indirect(idx3[:]), h1[:], gain1[:], ALU.mult)
 
         turned = {(b, q): held("turned%d%d" % (b, q), [P, 2, 2, P, 2], BF16) for b in range(2) for q in range(4)}
+
+        def hyd_rows(s):
+            return hyd_pairs[s // 2][:, s % 2, :]
 
         def scale_rows(rows, s):
             nc.scalar.activation(rows, rows, ACT.Copy, scale=factor[:, s:s + 1])
 
         def turned_part(s, q):
-            part = turned[s // 4, q][:, :, :, 32 * (s % 4):32 * (s % 4 + 1), :]
-            return part.rearrange("m k u q e -> m u k q e")
+            p0 = 32 * (s % SLICES_A_PASS)
+            return turned[s // SLICES_A_PASS, q][:, :, :, p0:p0 + 32, :].rearrange("m k u p e -> m u k p e")
 
-        def turn_sum(s, larger):
+        def turn_sum(s, larger, banks):
+            blocks = M // P // len(banks)
             for h in range(2):
-                half = slice(HALF * h, HALF * (h + 1))
-                scale_rows(larger[:, half], s)
-                acc = bank(3 + h, "turned_sum_%d_%d" % (s, h), [P, 4, P])
-                for term, rows in enumerate((hyd_rows(s)[:, half], larger[:, half])):
-                    for k in range(4):
+                scale_rows(larger[:, HALF * h:HALF * (h + 1)], s)
+            quarter_sums = []
+            for n, acc_bank in enumerate(banks):
+                acc = bank(acc_bank, "turned_sum_%d_%d" % (s, n), [P, blocks, P])
+                for term, rows in enumerate((hyd_rows(s), larger)):
+                    for k in range(blocks):
+                        c0 = P * (blocks * n + k)
                         nc.tensor.matmul(
-                            acc[:, k, :], rows[:, P * k:P * (k + 1)], ident[:],
-                            start=(term == 0 and k == 0), stop=(term == 1 and k == 3), is_transpose=True,
+                            acc[:, k, :], rows[:, c0:c0 + P], ident[:],
+                            start=(term == 0 and k == 0), stop=(term == 1 and k == blocks - 1), is_transpose=True,
                         )
-                for i in range(2):
-                    nc.scalar.copy(
-                        turned_part(s, 2 * h + i),
-                        acc[:, 2 * i:2 * (i + 1), :].rearrange("m k (q u e) -> m u k q e", u=2, e=2),
-                    )
+                quarter_sums.extend(acc[:, k:k + 2, :] for k in range(0, blocks, 2))
+            return quarter_sums
 
-        x_q = {}
+        def round_turned(s, quarter_sums):
+            for q, acc in enumerate(quarter_sums):
+                nc.scalar.copy(turned_part(s, q), acc.rearrange("m k (p u e) -> m u k p e", u=2, e=2))
 
-        def turn_back(b, q, acc_bank, engine_copy):
+        def turn_back(b, q, acc_bank, woven):
             words = turned[b, q][:].rearrange("m k u p e -> m k u (p e)").bitcast(F32)
-            woven = ring.tile([P, 4 * QUARTER], BF16, name="woven_%d_%d" % (b, q), tag="woven", bufs=4, align_bytes=64)
             acc = bank(acc_bank, "back_%d_%d" % (b, q), [P, 2, 2, P])
             for k in range(2):
                 for u in range(2):
                     nc.tensor.transpose(acc[:, k, u, :], words[:, k, u, :], ident[:])
-            dst = woven[:].bitcast(F32).rearrange("p (k m u) -> p k m u", k=2, u=2)
-            engine_copy(dst, acc[:].rearrange("p k u m -> p k m u"))
-            codes = held("x_codes_%d_%d" % (b, q), [P, QUARTER], U32)
-            scales = held("x_scales_%d_%d" % (b, q), [P, QUARTER], U8)
+            dst = woven.bitcast(F32).rearrange("p (k m u) -> p k m u", k=2, u=2)
+            nc.scalar.copy(dst, acc[:].rearrange("p k u m -> p k m u"))
+
+        x_q = {}
+
+        def quantise_x(b, q0, count, woven):
+            codes = held("x_codes_%d_%d" % (b, q0), [P, count * QUARTER], U32)
+            scales = held("x_scales_%d_%d" % (b, q0), [P, count * QUARTER], U8)
             nc.vector.quantize_mx(out=codes[:].bitcast(FP8X4), scales=scales[:], in_=woven[:])
-            x_q[b, q] = (codes, scales)
+            for i in range(count):
+                cols = slice(QUARTER * i, QUARTER * (i + 1))
+                x_q[b, q0 + i] = (codes[:, cols], scales[:, cols])
 
         h2 = {LEAD: make_h2(LEAD, whole, 2)}
         place_b(LEAD, whole, h2[LEAD])
-        h1 = {s: make_h1(s) for s in range(2)}
+        h1 = {0: make_h1(0, *make_sums(0))}
+        quantise_weights((2, 3), (), nc.scalar.copy, "grouped", "sum1_sb_0")
+        h1[1] = make_h1(1, *make_sums(1))
         scale_rows(hyd_rows(0), 0)
+        hyd_left = list(range(1, SLICES))
         for s in range(SLICES):
             place_a(s, h1[s])
-            if s in PLACE_B_AT:
-                place_b(PLACE_B_AT[s], whole, h2[PLACE_B_AT[s]])
-            if s in QUANTISE_AT:
-                quantise_weights(*QUANTISE_AT[s], nc.scalar.copy, *(("grouped", 2) if s == 0 else ("product", 2)))
-            if s + 2 < SLICES:
-                h1[s + 2] = make_h1(s + 2)
+            if s > 0 and s + LEAD < SLICES:
+                place_b(s + LEAD, whole, h2[s + LEAD])
+            w1_next = [n for n in (s + 3,) if n < SLICES and n not in w1_q]
+            w3_next = [n for n in (s + LEAD + 2,) if n < SLICES]
+            if w1_next or w3_next:
+                quantise_weights(w1_next, w3_next, nc.scalar.copy, "grouped" if s == 0 else "product")
+            if s + 2 < LAST:
+                h1[s + 2] = make_h1(s + 2, *make_sums(s + 2))
+            if s + 2 == LAST:
+                h1[LAST] = make_h1(LAST, *last_sums)
             if s + LEAD + 1 < SLICES:
                 h2[s + LEAD + 1] = make_h2(s + LEAD + 1, whole, 0)
             if s < LAST:
-                larger = slot(0, "larger_%d" % s, [P, M])
-                nc.vector.tensor_tensor(larger[:], page_a[s % PAGES_A][:], page_b[PAGE_OF[s]][:], ALU.max)
-                turn_sum(s, larger)
-            for ahead in HYD_AT.get(s, ()):
-                scale_rows(hyd_rows(ahead), ahead)
-            if s == 3:
-                for q in range(4):
-                    turn_back(0, q, 5 + q % 2, nc.scalar.copy)
+                larger = held("larger_%d" % s, [P, M], F32, "step")
+                nc.vector.tensor_tensor(larger[:], page_a[:], pages_b[s % PB_PAGES][:], ALU.max)
+                quarter_sums = turn_sum(s, larger, (3, 4, 5, 6) if s == LAST - 1 else (3, 4))
+                if s + 3 == LAST:
+                    last_sums = make_sums(LAST)
+                round_turned(s, quarter_sums)
+            count = 1 if s in (0, SLICES_A_PASS - 1) else 2
+            for n in hyd_left[:count]:
+                scale_rows(hyd_rows(n), n)
+            hyd_left = hyd_left[count:]
+            if s == SLICES_A_PASS - 1:
+                for h in range(2):
+                    woven_half = held("woven_half%d" % h, [P, 4 * HALF], BF16)
+                    for i in range(2):
+                        turn_back(0, 2 * h + i, 5 + i, woven_half[:, 4 * QUARTER * i:4 * QUARTER * (i + 1)])
+                    quantise_x(0, 2 * h, 2, woven_half)
 
-        larger = slot(0, "larger_last", [P, M])
+        larger = held("larger_last", [P, M], F32, "step")
         x_last = held("x_last", [P, M], BF16)
         quarters = [slice(QUARTER * q, QUARTER * (q + 1)) for q in range(4)]
-        for pair in (quarters[:2], quarters[2:]):
-            for cols in pair:
-                nc.vector.tensor_tensor(
-                    larger[:, cols], page_a[LAST % PAGES_A][:, cols], page_b[PAGE_OF[LAST]][:, cols], ALU.max,
-                )
-            for cols in pair:
+        for two in (quarters[:2], quarters[2:]):
+            for cols in two:
+                nc.vector.tensor_tensor(larger[:, cols], page_a[:, cols], pages_b[LAST % PB_PAGES][:, cols], ALU.max)
+            for cols in two:
                 nc.vector.scalar_tensor_tensor(
                     x_last[:, cols], larger[:, cols], factor[:, LAST:LAST + 1], hyd_rows(LAST)[:, cols], ALU.mult, ALU.add,
                 )
         for q in range(4):
-            acc = bank((3, 4, 3, 4)[q], "turned_last_%d" % q, [P, 2, P], BF16)
+            acc = bank(q % 2, "turned_last_%d" % q, [P, 2, P], BF16)
             for k in range(2):
                 nc.tensor.transpose(acc[:, k, :], x_last[:, QUARTER * q + P * k:QUARTER * q + P * (k + 1)], ident_bf[:])
             nc.scalar.copy(
                 turned_part(LAST, q).bitcast(F32),
-                acc[:].bitcast(F32).rearrange("m k (q u e) -> m u k q e", u=2, e=1),
+                acc[:].bitcast(F32).rearrange("m k (p u e) -> m u k p e", u=2, e=1),
             )
         for q in range(4):
-            turn_back(1, q, (5, 6, 5, 6)[q], nc.scalar.copy)
+            woven = ring.tile([P, 4 * QUARTER], BF16, name="woven_%d" % q, tag="woven", bufs=len(quarters), align_bytes=64)
+            turn_back(1, q, (2, 7)[q % 2], woven[:])
+            quantise_x(1, q, 1, woven)
 
-        out_banks = ((0, 1), (2, 7), (3, 4), (5, 6))
+        out_banks = ((3, 4), (5, 6), (0, 1), (2, 7))
         for q in range(4):
             sums = [bank(out_banks[q][pair], "out_%d_%d" % (q, pair), [P, 2, QUARTER]) for pair in range(2)]
             for b in range(2):
                 codes, scales = x_q[b, q]
-                for g in range(4):
-                    c0 = 512 * b + P * g
+                for g in range(N // P):
+                    c0 = N * b + P * g
                     nc.tensor.matmul_mx(
                         out=sums[g // 2][:, g % 2, :], lhsT=w4_w[:, 2 * c0:2 * (c0 + P)].bitcast(FP4X4),
-                        lhsT_scale=w4_sc[:, c0:c0 + P], rhs=codes[:].bitcast(FP8X4), rhs_scale=scales[:],
+                        lhsT_scale=w4_sc[:, c0:c0 + P], rhs=codes.bitcast(FP8X4), rhs_scale=scales,
                         start=(b == 0 and g % 2 == 0), stop=(b == 1 and g % 2 == 1),
                     )
             for pair in range(2):
-                rows = res_pairs[pair][:, :, quarters[q]]
-                result = ring.tile([P, 2, QUARTER], F32, name="result_%d_%d" % (q, pair), tag="w1_raw", bufs=8)
-                if (q, pair) in SCALAR_BANKS:
-                    staged = ring.tile([P, 2, QUARTER], F32, name="staged_%d_%d" % (q, pair), tag="first")
-                    nc.scalar.copy(staged[:], sums[pair][:])
-                    nc.gpsimd.tensor_tensor(result[:], staged[:], rows, ALU.add)
-                else:
-                    nc.vector.tensor_tensor(result[:], sums[pair][:], rows, ALU.add)
-                dst = out[256 * pair:256 * (pair + 1), quarters[q]].rearrange("(g p) m -> p g m", p=P)
+                result = ring.tile([P, 2, QUARTER], F32, name="result_%d_%d" % (q, pair), tag="w1_raw", bufs=W1_BUFS)
+                nc.vector.tensor_tensor(result[:], sums[pair][:], res_pairs[pair][:, :, quarters[q]], ALU.add)
+                dst = out[2 * P * pair:2 * P * (pair + 1), quarters[q]].rearrange("(g p) m -> p g m", p=P)
                 nc.sync.dma_start(dst, result[:])

from contextlib import ExitStack

import concourse.mybir as mybir
from concourse.masks import make_identity

F32 = mybir.dt.float32
BF16 = mybir.dt.bfloat16
I32 = mybir.dt.int32
U32 = mybir.dt.uint32
U16 = mybir.dt.uint16
U8 = mybir.dt.uint8
FP8X4 = mybir.dt.float8_e4m3fn_x4
FP4X4 = mybir.dt.float4_e2m1fn_x4
ALU = mybir.AluOpType
ACT = mybir.ActivationFunctionType

FLOPS = 3758096384

P = 128
T = 2048
S = 512
M = 1024
K_PASS = 512
H = 1024
N = 512
HALF = M // 2
QUARTER = M // 4
SLICES = H // P
LAST = SLICES - 1
SLICES_A_PASS = K_PASS // P
W3_PIECES = ((0, 128), (128, 384), (384, 640), (640, 1024))
W1_PIECES = ((0, 256), (256, 512), (512, 768), (768, 1024))
LEAD = 3
PB_PAGES = LEAD + 1
W1_BUFS = 7
ROW_BUFS = 4


def tile_list_gravimetry_storage_score_kernel(
    tc, tab_words, tab_scales, tab2_words, tab2_scales, offs, offs2, offs3, offs4,
    w1, w2_words, w2_scales, b1, w3, wg1, wg2, hyd, cal, w4_words, w4_scales, res, out,
):
    nc = tc.nc
    with ExitStack() as ctx:
        keep = ctx.enter_context(tc.tile_pool(name="keep", bufs=1))
        ring = ctx.enter_context(tc.tile_pool(name="ring", bufs=2))
        psum = ctx.enter_context(tc.psum_pool(name="psum", bufs=1))

        def held(name, shape, dtype, buffer=None):
            return keep.tile(shape, dtype, name=name, tag=buffer or name, align_bytes=64)

        def bank(index, name, shape, dtype=F32):
            return psum.tile(shape, dtype, name=name, tag="bank%d" % index)

        tab2_sc = held("tab2_sc", [P, T], U8)
        tab_sc = held("tab_sc", [P, 2 * T], U8)
        w2_sc = held("w2_sc", [P, 2 * H], U8)
        w4_sc = held("w4_sc", [P, 2 * N], U8)
        vector_rows = held("vector_rows", [P, P], F32)
        pages_b = [held("page_b%d" % i, [P, M], F32) for i in range(PB_PAGES)]
        page_a = held("page_a", [P, M], F32)
        nc.gpsimd.memset(tab2_sc[:].bitcast(I32), 0)
        nc.vector.memset(tab_sc[:].bitcast(I32), 0)
        nc.vector.memset(w2_sc[:].bitcast(I32), 0)
        nc.vector.memset(vector_rows[:], 0.0)
        nc.vector.memset(w4_sc[:].bitcast(I32), 0)
        for page in pages_b + [page_a]:
            nc.vector.memset(page[:], 0.0)
        ident = held("ident", [P, P], F32)
        make_identity(nc, ident[:])
        ident_bf = held("ident_bf", [P, P], BF16)
        make_identity(nc, ident_bf[:])

        def load_gain(name, src):
            tile = held(name, [P, S], F32)
            nc.sync.dma_start(tile[:], src)
            return tile

        def load_list(name, src):
            tile = keep.tile([P, S // 16], U16, name=name)
            nc.sync.dma_start(tile[:], src)
            return tile

        def load_weight(tag, bufs, w, a, c0, c1):
            src = w[K_PASS * a:K_PASS * (a + 1), c0:c1].rearrange("(p j) c -> p j c", j=4)
            tile = ring.tile([P, 4, c1 - c0], F32, name="%s_%d_%d" % (tag, a, c0), tag=tag, bufs=bufs)
            nc.sync.dma_start(tile[:], src)
            return tile

        def load_table_words(name, src):
            tile = held(name, [P, T], U32)
            nc.sync.dma_start(tile[:].bitcast(I32), src.rearrange("p c i -> p (c i)").bitcast(I32))
            return tile

        def load_scales(tile, src):
            passes = src.shape[0]
            for q in range(4):
                dst = tile[32 * q:32 * q + 4, :].bitcast(I32).rearrange("r (a c) -> r a c", a=passes)
                nc.sync.dma_start(dst, src[:, 4 * q:4 * q + 4, :].rearrange("a r c -> r a c").bitcast(I32))

        def load_fp4_words(name, src):
            tile = held(name, [P, 2 * src.shape[2]], U8)
            nc.sync.dma_start(
                tile[:].bitcast(I32).rearrange("p (a c) -> p a c", a=2),
                src.rearrange("a p c -> p a c").bitcast(I32),
            )
            return tile

        def load_row_pair(name, src, pair):
            rows = src[2 * P * pair:2 * P * (pair + 1), :].rearrange("(g p) m -> p g m", p=P)
            tile = ring.tile([P, 2, M], F32, name="%s%d" % (name, pair), tag="rows", bufs=ROW_BUFS)
            nc.sync.dma_start(tile[:], rows)
            return tile

        w1_raw, w3_raw, hyd_pairs = {}, {}, {}

        def load_w3(k):
            w3_raw[k] = [load_weight("w3_raw%d" % k, 1, w3, 0, *W3_PIECES[k])]

        def load_w1(k):
            w1_raw[k] = [load_weight("w1_raw", W1_BUFS, w1, a, *W1_PIECES[k]) for a in range(2)]

        idx2 = load_list("idx2", offs2)
        tab2_w = load_table_words("tab2_w", tab2_words[0])
        load_w3(0)
        load_w3(1)
        idx4 = load_list("idx4", offs4)
        idx3 = load_list("idx3", offs3)
        load_scales(tab2_sc, tab2_scales)
        gain2 = load_gain("gain2", wg2)
        load_w3(2)
        load_w1(0)
        nc.sync.dma_start(vector_rows[0:SLICES, :], b1.rearrange("(s p) -> s p", p=P))
        nc.sync.dma_start(vector_rows[SLICES:2 * SLICES, :], cal.rearrange("(s p) -> s p", p=P))
        tab_w = [load_table_words("tab_w%d" % a, tab_words[a]) for a in range(2)]
        load_scales(tab_sc, tab_scales)
        idx = load_list("idx", offs)
        load_w1(1)
        load_scales(w2_sc, w2_scales)
        w2_w = load_fp4_words("w2_w", w2_words)
        gain1 = load_gain("gain1", wg1)
        load_w3(3)
        hyd_pairs[0] = load_row_pair("hyd", hyd, 0)
        load_w1(2)
        hyd_pairs[1] = load_row_pair("hyd", hyd, 1)
        load_w1(3)
        hyd_pairs[2] = load_row_pair("hyd", hyd, 2)
        hyd_pairs[3] = load_row_pair("hyd", hyd, 3)
        w4_w = load_fp4_words("w4_w", w4_words)
        load_scales(w4_sc, w4_scales)
        res_pairs = [load_row_pair("res", res, pair) for pair in range(2)]

        turned_vectors = bank(7, "turned_vectors", [P, P])
        nc.tensor.transpose(turned_vectors[:], vector_rows[:], ident[:])
        vector_columns = held("vector_columns", [P, 2 * SLICES], F32)
        nc.scalar.copy(vector_columns[:], turned_vectors[:, 0:2 * SLICES])
        bias = vector_columns[:, 0:SLICES]
        factor = vector_columns[:, SLICES:2 * SLICES]

        def gather(dst, window, offsets):
            nc.vector.tensor_copy(dst, window.indirect(offsets))

        def slice_columns(raws, pieces, s):
            k = [c0 <= P * s < c1 for c0, c1 in pieces].index(True)
            c0 = P * s - pieces[k][0]
            return [raw[:, :, c0:c0 + P] for raw in raws[k]]

        w1_q, w3_q = {}, {}

        def quantise_weights(w1_slices, w3_slices, engine_copy, tag, codes_buffer=None):
            name = "w_%s_%s" % ("".join(map(str, w1_slices)), "".join(map(str, w3_slices)))
            parts = [part for s in w1_slices for part in slice_columns(w1_raw, W1_PIECES, s)]
            parts = parts + [part for s in w3_slices for part in slice_columns(w3_raw, W3_PIECES, s)]
            grouped = ring.tile([P, len(parts) * 4 * P], BF16, name=name + "_bf", tag=tag, align_bytes=64)
            for k, part in enumerate(parts):
                dst = grouped[:, 4 * P * k:4 * P * (k + 1)].rearrange("p (c i j) -> p c j i", i=4, j=4)
                engine_copy(dst, part.rearrange("p j (c i) -> p c j i", i=4))
            codes = held(name + "_codes", [P, len(parts) * P], U32, codes_buffer)
            scales = held(name + "_scales", [P, len(parts) * P], U8)
            nc.vector.quantize_mx(out=codes[:].bitcast(FP8X4), scales=scales[:], in_=grouped[:])
            operands = [(codes[:, P * k:P * (k + 1)], scales[:, P * k:P * (k + 1)]) for k in range(len(parts))]
            for k, s in enumerate(w1_slices):
                w1_q[s] = operands[2 * k:2 * k + 2]
            for k, s in enumerate(w3_slices):
                w3_q[s] = operands[2 * len(w1_slices) + k]

        v2_w = held("v2_w", [P, S], U32)
        v2_sc = held("v2_sc", [P, S], U8)

        def make_h2(s, entries, acc_bank):
            count = entries.stop - entries.start
            acc = bank(acc_bank, "sum3_%d_%d" % (s, entries.start), [P, count])
            codes, scales = w3_q[s]
            nc.tensor.matmul_mx(
                out=acc[:], lhsT=codes.bitcast(FP8X4), lhsT_scale=scales,
                rhs=v2_w[:, entries].bitcast(FP8X4), rhs_scale=v2_sc[:, entries], start=True, stop=True,
            )
            if s == LEAD:
                h2 = held("h2_lead", [P, count], F32, "tab_sc")
            else:
                h2 = ring.tile([P, count], F32, name="h2_%d_%d" % (s, entries.start), tag="h2")
            nc.scalar.activation(h2[:], acc[:], ACT.Tanh)
            return h2

        def place_b(s, entries, h2):
            offsets = idx4[:, entries.start // 16:entries.stop // 16]
            nc.vector.tensor_tensor(pages_b[s % PB_PAGES][:].indirect(offsets), h2[:], gain2[:, entries], ALU.mult)

        list_halves = [slice(S // 2 * e, S // 2 * (e + 1)) for e in range(2)]
        for entries in list_halves:
            gather(v2_w[:, entries], tab2_w[:], idx2[:, entries.start // 16:entries.stop // 16])
        quantise_weights((), range(LEAD), nc.vector.tensor_copy, "grouped")
        for entries in list_halves:
            gather(v2_sc[:, entries], tab2_sc[:], idx2[:, entries.start // 16:entries.stop // 16])
        for e, entries in enumerate(list_halves):
            place_b(0, entries, make_h2(0, entries, 2 + e))
        whole = slice(0, S)
        for s in range(1, LEAD):
            place_b(s, whole, make_h2(s, whole, 2))
        quantise_weights((), (LEAD, LEAD + 1), nc.scalar.copy, "grouped")
        quantise_weights((0, 1), (), nc.scalar.copy, "grouped")

        v_sc = [held("v_sc%d" % a, [P, S], U8) for a in range(2)]
        v_w = [held("v_w%d" % a, [P, S], U32) for a in range(2)]
        for a in range(2):
            gather(v_sc[a][:], tab_sc[:, T * a:T * (a + 1)], idx[:])
        for a in range(2):
            gather(v_w[a][:], tab_w[a][:], idx[:])

        def make_sums(s):
            acc1 = bank(1 if s in (1, 2) else 0, "sum1_%d" % s, [P, S])
            acc2 = bank({0: 1, 1: 7, 2: 2}.get(s, (7, 1)[s % 2]), "sum2_%d" % s, [P, S])
            for a in range(2):
                codes, scales = w1_q[s][a]
                nc.tensor.matmul_mx(
                    out=acc1[:], lhsT=codes.bitcast(FP8X4), lhsT_scale=scales,
                    rhs=v_w[a][:].bitcast(FP8X4), rhs_scale=v_sc[a][:], start=(a == 0), stop=(a == 1),
                )
            for a in range(2):
                c0 = H * a + P * s
                nc.tensor.matmul_mx(
                    out=acc2[:], lhsT=w2_w[:, 2 * c0:2 * (c0 + P)].bitcast(FP4X4), lhsT_scale=w2_sc[:, c0:c0 + P],
                    rhs=v_w[a][:].bitcast(FP8X4), rhs_scale=v_sc[a][:], start=(a == 0), stop=(a == 1),
                )
            sum1 = held("sum1_sb_%d" % s, [P, S], F32, "step" if s >= 2 else None)
            nc.scalar.copy(sum1[:], acc1[:])
            return sum1, acc2

        def make_h1(s, sum1, acc2):
            if s == 0:
                product = held("product_0", [P, S], F32)
            else:
                product = ring.tile([P, S], F32, name="product_%d" % s, tag="product", align_bytes=64)
            nc.vector.tensor_tensor(product[:], acc2[:], sum1[:], ALU.mult)
            h1 = ring.tile([P, S], F32, name="h1_%d" % s, tag="h1")
            nc.scalar.activation(h1[:], product[:], ACT.Identity, bias=bias[:, s:s + 1], scale=1.0)
            return h1

        def place_a(s, h1):
            nc.vector.tensor_tensor(page_a[:].indirect(idx3[:]), h1[:], gain1[:], ALU.mult)

        turned = {(b, q): held("turned%d%d" % (b, q), [P, 2, 2, P, 2], BF16) for b in range(2) for q in range(4)}

        def hyd_rows(s):
            return hyd_pairs[s // 2][:, s % 2, :]

        def scale_rows(rows, s):
            nc.scalar.activation(rows, rows, ACT.Copy, scale=factor[:, s:s + 1])

        def turned_part(s, q):
            p0 = 32 * (s % SLICES_A_PASS)
            return turned[s // SLICES_A_PASS, q][:, :, :, p0:p0 + 32, :].rearrange("m k u p e -> m u k p e")

        def turn_sum(s, larger, banks):
            blocks = M // P // len(banks)
            for h in range(2):
                scale_rows(larger[:, HALF * h:HALF * (h + 1)], s)
            quarter_sums = []
            for n, acc_bank in enumerate(banks):
                acc = bank(acc_bank, "turned_sum_%d_%d" % (s, n), [P, blocks, P])
                for term, rows in enumerate((hyd_rows(s), larger)):
                    for k in range(blocks):
                        c0 = P * (blocks * n + k)
                        nc.tensor.matmul(
                            acc[:, k, :], rows[:, c0:c0 + P], ident[:],
                            start=(term == 0 and k == 0), stop=(term == 1 and k == blocks - 1), is_transpose=True,
                        )
                quarter_sums.extend(acc[:, k:k + 2, :] for k in range(0, blocks, 2))
            return quarter_sums

        def round_turned(s, quarter_sums):
            for q, acc in enumerate(quarter_sums):
                nc.scalar.copy(turned_part(s, q), acc.rearrange("m k (p u e) -> m u k p e", u=2, e=2))

        def turn_back(b, q, acc_bank, woven):
            words = turned[b, q][:].rearrange("m k u p e -> m k u (p e)").bitcast(F32)
            acc = bank(acc_bank, "back_%d_%d" % (b, q), [P, 2, 2, P])
            for k in range(2):
                for u in range(2):
                    nc.tensor.transpose(acc[:, k, u, :], words[:, k, u, :], ident[:])
            dst = woven.bitcast(F32).rearrange("p (k m u) -> p k m u", k=2, u=2)
            nc.scalar.copy(dst, acc[:].rearrange("p k u m -> p k m u"))

        x_q = {}

        def quantise_x(b, q0, count, woven):
            codes = held("x_codes_%d_%d" % (b, q0), [P, count * QUARTER], U32)
            scales = held("x_scales_%d_%d" % (b, q0), [P, count * QUARTER], U8)
            nc.vector.quantize_mx(out=codes[:].bitcast(FP8X4), scales=scales[:], in_=woven[:])
            for i in range(count):
                cols = slice(QUARTER * i, QUARTER * (i + 1))
                x_q[b, q0 + i] = (codes[:, cols], scales[:, cols])

        h2 = {LEAD: make_h2(LEAD, whole, 2)}
        place_b(LEAD, whole, h2[LEAD])
        h1 = {0: make_h1(0, *make_sums(0))}
        quantise_weights((2, 3), (), nc.scalar.copy, "grouped", "sum1_sb_0")
        h1[1] = make_h1(1, *make_sums(1))
        scale_rows(hyd_rows(0), 0)
        hyd_left = list(range(1, SLICES))
        for s in range(SLICES):
            place_a(s, h1[s])
            if s > 0 and s + LEAD < SLICES:
                place_b(s + LEAD, whole, h2[s + LEAD])
            w1_next = [n for n in (s + 3,) if n < SLICES and n not in w1_q]
            w3_next = [n for n in (s + LEAD + 2,) if n < SLICES]
            if w1_next or w3_next:
                quantise_weights(w1_next, w3_next, nc.scalar.copy, "grouped" if s == 0 else "product")
            if s + 2 < LAST:
                h1[s + 2] = make_h1(s + 2, *make_sums(s + 2))
            if s + 2 == LAST:
                h1[LAST] = make_h1(LAST, *last_sums)
            if s + LEAD + 1 < SLICES:
                h2[s + LEAD + 1] = make_h2(s + LEAD + 1, whole, 0)
            if s < LAST:
                larger = held("larger_%d" % s, [P, M], F32, "step")
                nc.vector.tensor_tensor(larger[:], page_a[:], pages_b[s % PB_PAGES][:], ALU.max)
                quarter_sums = turn_sum(s, larger, (3, 4, 5, 6) if s == LAST - 1 else (3, 4))
                if s + 3 == LAST:
                    last_sums = make_sums(LAST)
                round_turned(s, quarter_sums)
            count = 1 if s in (0, SLICES_A_PASS - 1) else 2
            for n in hyd_left[:count]:
                scale_rows(hyd_rows(n), n)
            hyd_left = hyd_left[count:]
            if s == SLICES_A_PASS - 1:
                for h in range(2):
                    woven_half = held("woven_half%d" % h, [P, 4 * HALF], BF16)
                    for i in range(2):
                        turn_back(0, 2 * h + i, 5 + i, woven_half[:, 4 * QUARTER * i:4 * QUARTER * (i + 1)])
                    quantise_x(0, 2 * h, 2, woven_half)

        larger = held("larger_last", [P, M], F32, "step")
        x_last = held("x_last", [P, M], BF16)
        quarters = [slice(QUARTER * q, QUARTER * (q + 1)) for q in range(4)]
        for two in (quarters[:2], quarters[2:]):
            for cols in two:
                nc.vector.tensor_tensor(larger[:, cols], page_a[:, cols], pages_b[LAST % PB_PAGES][:, cols], ALU.max)
            for cols in two:
                nc.vector.scalar_tensor_tensor(
                    x_last[:, cols], larger[:, cols], factor[:, LAST:LAST + 1], hyd_rows(LAST)[:, cols], ALU.mult, ALU.add,
                )
        for q in range(4):
            acc = bank(q % 2, "turned_last_%d" % q, [P, 2, P], BF16)
            for k in range(2):
                nc.tensor.transpose(acc[:, k, :], x_last[:, QUARTER * q + P * k:QUARTER * q + P * (k + 1)], ident_bf[:])
            nc.scalar.copy(
                turned_part(LAST, q).bitcast(F32),
                acc[:].bitcast(F32).rearrange("m k (p u e) -> m u k p e", u=2, e=1),
            )
        for q in range(4):
            woven = ring.tile([P, 4 * QUARTER], BF16, name="woven_%d" % q, tag="woven", bufs=len(quarters), align_bytes=64)
            turn_back(1, q, (2, 7)[q % 2], woven[:])
            quantise_x(1, q, 1, woven)

        out_banks = ((3, 4), (5, 6), (0, 1), (2, 7))
        for q in range(4):
            sums = [bank(out_banks[q][pair], "out_%d_%d" % (q, pair), [P, 2, QUARTER]) for pair in range(2)]
            for b in range(2):
                codes, scales = x_q[b, q]
                for g in range(N // P):
                    c0 = N * b + P * g
                    nc.tensor.matmul_mx(
                        out=sums[g // 2][:, g % 2, :], lhsT=w4_w[:, 2 * c0:2 * (c0 + P)].bitcast(FP4X4),
                        lhsT_scale=w4_sc[:, c0:c0 + P], rhs=codes.bitcast(FP8X4), rhs_scale=scales,
                        start=(b == 0 and g % 2 == 0), stop=(b == 1 and g % 2 == 1),
                    )
            for pair in range(2):
                result = ring.tile([P, 2, QUARTER], F32, name="result_%d_%d" % (q, pair), tag="w1_raw", bufs=W1_BUFS)
                nc.vector.tensor_tensor(result[:], sums[pair][:], res_pairs[pair][:, :, quarters[q]], ALU.add)
                dst = out[2 * P * pair:2 * P * (pair + 1), quarters[q]].rearrange("(g p) m -> p g m", p=P)
                nc.sync.dma_start(dst, result[:])
